import numpy as np, ml_dtypes
CORES = [2,3,42,43,82,83,122,123]
N = 8
BF = ml_dtypes.bfloat16
def gentries(a):
    return np.ascontiguousarray(a.reshape(8, 16, -1).transpose(0, 2, 1)).reshape(8, -1)
def gtable(e):
    e = np.asarray(e); return np.ascontiguousarray(e.reshape(8, -1, 16).transpose(0, 2, 1)).reshape(128, -1).astype(np.int32)
V, CAP, D, R = 32, 8, 6, 2
def cube():
    P = np.indices((4, 4, 4, 4)).reshape(4, -1).T; P = P[(np.sort(P, 1) == np.arange(4)).all(1)]
    w = np.array([64, 16, 4, 1]); at = np.zeros(256, np.int64); at[P @ w] = np.arange(24)
    return at[P[:, P] @ w]
def cyclic():
    i = np.arange(24); return (i[:, None] + i) % 24
def dihedral():
    i = np.arange(24); r = i % 12; s = i // 12
    return (r[:, None] + np.where(s[:, None] == 1, -r, r)) % 12 + 12 * (s[:, None] ^ s)
def labelled(rng, plain=0, mixed=False):
    res = np.zeros((8, 24, 24), np.int64)
    for g in range(8):
        c = cyclic() if mixed and g in (2, 3) else dihedral() if mixed and g in (4, 5) else cube()
        lab = np.arange(24) if g < plain else rng.permutation(24)
        res[g][lab[:, None], lab[None, :]] = lab[c]
    return res
def values(rng):
    return rng.standard_normal((N, 128, V * 24), dtype=np.float32) * np.exp2(rng.integers(-2, 3, (N, 128, 1))).astype(np.float32)
def raw(rng, plain=0, mixed=False):
    q = (np.arange(N)[:, None, None, None] + 1 + rng.integers(0, N - 1, (N, 8, D, V))) % N
    slot = V + q * CAP + rng.integers(0, CAP, (N, 8, D, V)); own = rng.integers(0, V, (N, 8, D, V))
    return {"x": values(rng), "pose": rng.integers(0, 24, (N, 8, V)), "act": rng.integers(0, 24, (N, 8, R - 1, V)), "c": labelled(rng, plain, mixed),
            "shown": np.argsort(rng.random((N, 8, N, V)), -1)[..., :CAP], "nbr": np.where(rng.random((N, 8, D, V)) < 0.5, own, slot)}
def glists(a):
    return np.stack([gtable(v.reshape(8, -1)) for v in a])
def pack(d):
    c = d["c"]; rel = np.argsort(c, 2).transpose(0, 2, 1)
    every = lambda t: np.repeat(np.ascontiguousarray(t).reshape(1, 8, 576).astype(np.int32), N, 0)
    return {"x": np.ascontiguousarray(d["x"].astype(np.float32)), "pose": glists(d["pose"]), "act": glists(d["act"]), "rel": every(rel), "ct": every(c), "shown": glists(d["shown"]), "nbr": glists(d["nbr"])}
def setup_inputs(rng):
    return pack(raw(rng))
def setup_inputs_full(rng):
    d = raw(rng, mixed=True)
    for r in range(N):
        s = np.concatenate([V + q * CAP + np.arange(CAP) for q in range(N) if q != r])
        for g in range(8):
            flat = d["nbr"][r, g].reshape(-1).copy(); flat[rng.permutation(D * V)[:len(s)]] = s; d["nbr"][r, g] = flat.reshape(D, V)
    return pack(d)
def setup_inputs_repeat(rng):
    d = raw(rng); a, b, e, w = rng.permutation(N)[:4]; n = d["nbr"]
    n[a] = rng.integers(0, V, (8, D, V)); n[a, :, 0] = np.arange(V)
    n[b] = V + a * CAP + rng.integers(0, CAP, (8, D, V))
    n[e] = n[e][:, :1]; q0 = 1 if e == 0 else 0; q1 = N - 2 if e == N - 1 else N - 1
    n[e, :, :, 0] = 0; n[e, :, :, V - 1] = V - 1; n[e, :, :, 1] = V + q1 * CAP + CAP - 1; n[e, :, :, 2] = V + q0 * CAP
    d["shown"][w] = d["shown"][w][..., :1]
    return pack(d)
def setup_inputs_below(rng):
    d = raw(rng); k = rng.integers(0, 87, 8); k[rng.integers(0, 8)] = 86
    d["x"] = -rng.integers(1, 200, (N, 128, V * 24)).astype(np.float32) * np.repeat(np.exp2(k), 16)[:, None].astype(np.float32); return pack(d)
def setup_inputs_alike(rng):
    d = raw(rng, 2, True)
    for g in range(8):
        if g % 2 == 0:
            d["pose"][:, g] = rng.integers(0, 24); d["act"][:, g] = rng.integers(0, 24, (1, R - 1, 1))
        else:
            d["act"][:, g] = np.argmax((d["c"][g] == np.arange(24)).all(1))
    return pack(d)
def setup_inputs_spread(rng):
    d = raw(rng); k = (N, 1, V * 24)
    d["x"] = d["x"] * (np.exp2(rng.integers(-6, 7, k)) * (rng.random(k) > 0.0625)).astype(np.float32); return pack(d)
def check_inputs(d):
    bad = []; j = np.arange(24)
    def within(a, top): return bool((a >= 0).all() and (a < top).all())
    if not np.isfinite(d["x"]).all(): bad.append("finite")
    elif not (np.abs(d["x"]) <= 2.0 ** 94).all(): bad.append("size")
    if not within(d["pose"], 24): bad.append("pose")
    if not within(d["act"], 24): bad.append("act")
    if not within(d["shown"], V): bad.append("shown")
    for r in range(N):
        n = d["nbr"][r]
        if not within(n, V + N * CAP) or ((n >= V + r * CAP) & (n < V + r * CAP + CAP)).any(): bad.append("nbr"); break
    if not (d["rel"] == d["rel"][:1]).all() or not (d["ct"] == d["ct"][:1]).all(): bad.append("tables_alike")
    if not within(d["rel"], 24) or not within(d["ct"], 24): bad.append("tables_range")
    else:
        for g in range(8):
            c = d["ct"][0, g].reshape(24, 24).astype(np.int64); l = d["rel"][0, g].reshape(24, 24).astype(np.int64)
            if not ((np.sort(c, 1) == j).all() and (np.sort(c, 0) == j[:, None]).all() and (c[c] == c[:, c]).all()): bad.append("ct_group"); break
            if not (c[j[None, :], l] == j[:, None]).all(): bad.append("rel"); break
    return bad
def reference(x, pose, act, rel, ct, shown, nbr):
    f = x.reshape(N, 8, 16, V, 24)
    p = np.stack([gentries(v) for v in pose]).astype(np.int64)
    ac = np.stack([gentries(v) for v in act]).reshape(N, 8, R - 1, V).astype(np.int64)
    sh = np.stack([gentries(v) for v in shown]).reshape(N, 8, N, CAP)
    nb = np.stack([gentries(v) for v in nbr]).reshape(N, 8, D, V)
    for t in range(R):
        new = np.zeros(f.shape, np.float32); turned = np.zeros(p.shape, np.int64)
        for r in range(N):
            for g in range(8):
                fe = np.concatenate([f[r, g]] + [f[q, g][:, sh[q, g, r]] for q in range(N)], 1)
                pe = np.concatenate([p[r, g]] + [p[q, g][sh[q, g, r]] for q in range(N)])
                j = nb[r, g]
                e = rel[r, g][p[r, g][None, :] * 24 + pe[j]].astype(np.int64)
                k = ct[r, g][e[:, :, None] * 24 + np.arange(24)]
                new[r, g] = np.maximum.reduce(fe[:, j[:, :, None], k], axis=1)
                if t < R - 1: turned[r, g] = ct[r, g][p[r, g] * 24 + ac[r, g, t]]
        f = new; p = turned
    return {"y": np.ascontiguousarray(f.reshape(N, 128, V * 24))}

@@ -1,0 +1,417 @@
+from concourse.bass import DstId, RemoteDMATransfer
+from concourse.mybir import AluOpType as OP, AxisListType, ActivationFunctionType as AF
+
+NR, CH, M = 8, 2, 12
+OWN, REG = 32 * M, 8 * M
+WIN = OWN + NR * REG
+RK = [(r, k) for r in range(2) for k in range(CH)]
+RELAY = {(0, 0): True, (0, 1): True, (1, 0): True, (1, 1): True}
+
+F32, I32, U16, B16 = "float32", "int32", "uint16", "bfloat16"
+SCRATCH = {
+    "xs": ("sbuf", [128, 768], F32), "n0": ("sbuf", [128, 768], F32), "n1": ("sbuf", [128, 768], F32),
+    "yp": ("sbuf", [128, 768], F32), "ys": ("sbuf", [128, 768], F32),
+    "ts": ("sbuf", [128, 128], I32), "tt": ("sbuf", [128, 128], I32), "tabr": ("sbuf", [128, 64], B16),
+    "tabc": ("sbuf", [128, 64], B16), "tabt": ("sbuf", [128, 64], B16),
+    "prow": ("sbuf", [128, 256], I32), "rowe": ("sbuf", [128, 256], B16),
+    "shi": ("sbuf", [128, 4], I32), "shb": ("sbuf", [128, 4], B16),
+    "nb": ("sbuf", [128, 12], I32), "acti": ("sbuf", [128, 2], I32), "posi": ("sbuf", [128, 2], I32),
+    "actf": ("sbuf", [128, 2], F32), "posf": ("sbuf", [128, 2], F32),
+    "ones": ("sbuf", [128, 128], B16), "idf": ("sbuf", [128, 128], F32), "idb": ("sbuf", [128, 128], B16),
+    "rt": ("sbuf", [128, 128], F32), "rp": ("sbuf", [128, 256], B16),
+    "pidx": ("sbuf", [128, 2], I32), "ri": ("sbuf", [128, 2], I32), "wi": ("sbuf", [128, 2], I32), "gi": ("sbuf", [128, 2], I32),
+    "i24": ("sbuf", [128, 2], F32), "r16": ("sbuf", [128, 2], F32), "w32": ("sbuf", [128, 2], F32), "g32": ("sbuf", [128, 2], F32),
+    "g16": ("sbuf", [128, 2], F32),
+    "kcol": ("sbuf", [128, 2], F32), "rc": ("sbuf", [128, 256], F32), "cwi": ("sbuf", [128, M // 2], F32), "cw": ("sbuf", [128, M // 2], F32),
+    "u24": ("sbuf", [128, 24], F32), "jt": ("sbuf", [128, 48], I32), "jj": ("sbuf", [128, 48], I32), "jm": ("sbuf", [128, 48], I32),
+    "ji": ("sbuf", [128, 48], I32), "ja": ("sbuf", [128, 48], F32), "jb": ("sbuf", [128, 48], F32), "jc": ("sbuf", [128, 48], F32),
+    "lc": ("sbuf", [128, 48], U16), "lf0": ("sbuf", [128, 48], U16), "lf1": ("sbuf", [128, 48], U16), "ly": ("sbuf", [128, 48], U16),
+    "l0": ("sbuf", [128, 7 * (M // 2) + 6], U16), "ln": ("sbuf", [128, 6 * 2 * M], U16),
+    "oh": ("sbuf", [128, 512], B16), "oh2": ("sbuf", [128, 512], B16), "oh3": ("sbuf", [128, 512], B16),
+    "dg2": ("sbuf", [128, 256], B16), "dg3": ("sbuf", [128, 256], B16),
+    "hi": ("sbuf", [128, 12], I32), "lo": ("sbuf", [128, 12], I32), "own": ("sbuf", [128, 12], F32), "st": ("sbuf", [128, 12], F32),
+    "sb0": ("sbuf", [128, 12], F32), "sb1": ("sbuf", [128, 12], F32), "df": ("sbuf", [128, 12], F32), "dg": ("sbuf", [128, 12], F32),
+    "base": ("sbuf", [128, 12], F32),
+    "mk": ("sbuf", [128, 64], F32), "mx": ("sbuf", [128, 64], F32), "a1": ("sbuf", [128, 2], F32), "a1e": ("sbuf", [128, 2], F32),
+    "mk2": ("sbuf", [128, 64], F32), "mx2": ("sbuf", [128, 64], F32), "k1": ("sbuf", [128, 2], F32), "k1e": ("sbuf", [128, 2], F32),
+}
+for _n in ("pb1", "psa", "psb", "pss", "pb2", "psc", "pb3", "psd"):
+    SCRATCH[_n] = ("psum", [128, 512], F32)
+for _r, _k in RK:
+    SCRATCH["w%d%d" % (_r, _k)] = ("sbuf", [128, WIN], F32)
+    SCRATCH["s%d%d" % (_r, _k)] = ("sbuf", [128, 7 * REG], F32)
+    SCRATCH["q%d%d" % (_r, _k)] = ("sbuf", [128, OWN], F32)
+    SCRATCH["rl%d%d" % (_r, _k)] = ("sbuf", [128, 2 * REG], F32)
+SEMAPHORES = ["ms", "one", "vown", "i1", "i2", "i3", "i4", "i5", "c1", "c2", "c3", "c4", "c5", "j1", "j2", "j3", "j4", "j5",
+              "dp", "ds", "dr", "dx", "dc", "dm", "dy", "row", "pb", "shc", "pS", "tr", "tab", "ohc", "pA", "pB", "vl0", "vlf",
+              "ctr", "ctb", "afc", "m1", "m2", "m3", "m4", "d2", "p2", "o2", "pC", "vly", "e1", "e2", "e3", "e4", "d3", "p3", "o3", "pD", "vl1",
+              "b1", "b2", "b3", "b4", "b5", "b6", "b7", "y1", "y2a", "y2b", "lsem"]
+for _r, _k in RK:
+    SEMAPHORES += [_s + "%d%d" % (_r, _k) for _s in ("f", "s", "t", "arr", "rel", "na", "nb", "aa", "ab")]
+
+
+def routes(src, rk, T, topo):
+    cores = T.cores
+    c = cores[src]
+    here = [p for p in range(NR) if p != src and topo.chip(cores[p]) == topo.chip(c)]
+    away = [p for p in range(NR) if p != src and p not in here]
+
+    def place(p):
+        return sum(1 for q in range(p) if topo.chip(cores[q]) == topo.chip(cores[p]))
+    relay = [p for p in away if not topo.same_plane(topo.chip(c), topo.chip(cores[p])) and place(p) == place(src)] if RELAY[rk] else []
+    direct = [p for p in away if p not in relay]
+    helper = None
+    if relay:
+        ok = [h for h in topo.cores_of(c) if topo.die(h) != topo.die(c) and all(topo.may_write(h, cores[p]) for p in relay)]
+        helper = ok[place(src)]
+    return direct, relay, here, helper
+
+
+def calls(src, rk, T, topo):
+    cores = T.cores
+    direct, relay, here, helper = routes(src, rk, T, topo)
+    c = cores[src]
+    off = topo.engines(c, cores[direct[0]])
+    rest = [e for e in topo.engines(c, cores[here[0]]) if e not in off]
+    res = []
+    while direct:
+        part, direct = direct[:4], direct[4:]
+        n = len(off) // len(part)
+        call = [(p, cores[p], off[n * i:n * i + n]) for i, p in enumerate(part)]
+        if relay:
+            m = len(rest) // len(relay)
+            call += [(p, helper, rest[m * i:m * i + m]) for i, p in enumerate(relay)]
+            relay = []
+        res.append(call)
+    res.append([(p, cores[p], rest) for p in here])
+    return res
+
+
+def hand_on(src, rk, T, topo):
+    _, relay, _, helper = routes(src, rk, T, topo)
+    if not relay:
+        return []
+    off = topo.engines(helper, T.cores[relay[0]])
+    n = len(off) // len(relay)
+    return [(p, off[n * i:n * i + n]) for i, p in enumerate(relay)]
+
+
+def bits(engines):
+    return sum(1 << e for e in engines)
+
+
+def transfer(topo, dst, out, src, sem, engines):
+    rid, pid, _ = topo.addr(dst)
+    return RemoteDMATransfer(dst_ids=[DstId(rid=rid, pnc=pid)], dma_engine_mask=bits(engines), remote_sem=sem, src=src, dst=out)
+
+
+def helper_program(g, core, T, topo):
+    sent = 0
+    for r, k in RK:
+        tag = "%d%d" % (r, k)
+        for src in range(NR):
+            if routes(src, (r, k), T, topo)[3] != core:
+                continue
+            inc = sum(len(e) for call in calls(src, (r, k), T, topo) for p, c, e in call if c == core)
+            out = hand_on(src, (r, k), T, topo)
+            g.wait_ge(T.sem["rel" + tag], inc)
+            at = OWN + REG * src
+            g.remote_dma_fused([transfer(topo, T.cores[p], T["w" + tag][:, at:at + REG], T["rl" + tag][:, REG * i:REG * i + REG],
+                                         T.sem["arr" + tag], e) for i, (p, e) in enumerate(out)], local_sem=T.sem["lsem"])
+            sent += sum(len(e) for p, e in out)
+    if sent:
+        g.wait_ge(T.sem["lsem"], sent)
+
+
+def rank_program(g, core, T, topo):
+    rank = T.rank_of(core)
+    if rank is None:
+        helper_program(g, core, T, topo)
+        return
+    V, S, TE, Y = g.vector, g.scalar, g.tensor, g.sync
+    cnt, seen = {}, {}
+
+    def sg(name, inst, n=1):
+        inst.then_inc(T.sem[name], n)
+        cnt[name] = cnt.get(name, 0) + n
+
+    def wt(q, *names):
+        for name in names:
+            q.wait_ge(T.sem[name], cnt[name])
+            seen[name] = cnt[name]
+
+    def tsc(sem, out, in0, s1, op0, s2=None, op1=None):
+        if op1 is None:
+            sg(sem, V.tensor_scalar(out, in0, s1, None, op0))
+        else:
+            sg(sem, V.tensor_scalar(out, in0, s1, s2, op0, op1))
+
+    def ttn(sem, out, a, b, op):
+        sg(sem, V.tensor_tensor(out, a, b, op))
+
+    sg("ms", V.memset(T.ts[:, :], 0))
+    sg("one", V.memset(T.ones[:, :], 1.0))
+    sg("dp", Y.dma_start(T.prow[0:1, 0:256], T.pose[:, :]), 16)
+    sg("ds", S.dma_start(T.shi[:, :], T.shown[:, :]), 16)
+    wt(Y, "ms")
+    wt(S, "ms")
+    for t in range(2):
+        for gg in range(4):
+            q = Y if gg < 2 else S
+            sg("dr", q.dma_start(T.ts[32 * gg:32 * gg + 24, 32 * t:32 * t + 24], T.rel[4 * t + gg:4 * t + gg + 1, :]), 16)
+    sg("dx", Y.dma_start(T.xs[:, :], T.x[:, :]), 16)
+    for t in range(2):
+        for gg in range(4):
+            q = Y if gg < 2 else S
+            sg("dc", q.dma_start(T.ts[32 * gg:32 * gg + 24, 64 + 32 * t:64 + 32 * t + 24], T.ct[4 * t + gg:4 * t + gg + 1, :]), 16)
+    sg("dm", S.dma_start(T.nb[:, :], T.nbr[:, :]), 16)
+    sg("dm", S.dma_start(T.acti[:, :], T.act[:, :]), 16)
+    sg("dm", S.dma_start(T.posi[:, :], T.pose[:, :]), 16)
+
+    def iota(sem, out, pattern, cm, flag=True):
+        if flag:
+            sg(sem, g.iota(out, pattern, 0, cm, allow_small_or_imprecise_dtypes=True))
+        else:
+            sg(sem, g.iota(out, pattern, 0, cm))
+    iota("i1", T.pidx[:, 0:1], [[0, 1]], 1, False)
+    iota("i2", T.rt[:, :], [[-16, 8], [0, 2], [-1, 8]], 1)
+    iota("i3", T.cwi[:, :], [[64, M // 2]], 0)
+    iota("i3", T.rc[0:1, :], [[0, 2], [32, 8], [0, 16]], 0)
+    iota("i3", T.kcol[:, :], [[128, 2]], 1)
+    iota("i4", T.u24[:, :], [[1, 24]], 0)
+    iota("i4", T.idf[:, :], [[-1, 128]], 1)
+    iota("i5", T.jt[:, :], [[16, 48]], 1, False)
+
+    wt(V, "i1")
+    p1 = T.pidx[:, 0:1]
+    tsc("c1", T.ri[:, 0:1], p1, 15, OP.bitwise_and)
+    tsc("c1", T.wi[:, 0:1], p1, 3, OP.arith_shift_right, 1, OP.bitwise_and)
+    tsc("c1", T.gi[:, 0:1], p1, 4, OP.arith_shift_right)
+    wt(V, "i2")
+    for v in range(2):
+        tsc("c3", T.rp[:, 128 * v:128 * v + 128], T.rt[:, :], 8.0 * v, OP.is_equal)
+    wt(V, "c1")
+    for q in range(2):
+        tsc("c2", T.i24[:, q:q + 1], T.ri[:, 0:1], 24.0, OP.mult, 384.0 * q, OP.add)
+        tsc("c2", T.r16[:, q:q + 1], T.ri[:, 0:1], 16.0 * q, OP.add)
+    tsc("c2", T.w32[:, 0:1], T.wi[:, 0:1], 32.0, OP.mult)
+    tsc("c2", T.g32[:, 0:1], T.gi[:, 0:1], 32.0, OP.mult)
+    tsc("c2", T.g16[:, 0:1], T.gi[:, 0:1], 16.0, OP.mult)
+    wt(V, "i3", "c2")
+    tsc("c4", T.cw[:, :], T.cwi[:, :], T.w32[:, 0:1], OP.add)
+
+    wt(V, "dp")
+    for q in range(2):
+        ttn("row", T.rowe[0:1, 128 * q:128 * q + 128], T.prow[0:1, q:256:2], T.rc[0:1, 128 * q:128 * q + 128], OP.add)
+    wt(TE, "row", "one")
+    sg("pb", TE.matmul(T.pb1[:, 0:256], T.ones[0:1, 0:128], T.rowe[0:1, 0:256], True, True))
+    wt(V, "ds")
+    sg("shc", V.tensor_copy(T.shb[:, :], T.shi[:, :]))
+    wt(TE, "shc", "c3")
+    for v in range(2):
+        sg("pS", TE.matmul(T.pss[:, 4 * v:4 * v + 4], T.rp[:, 128 * v:128 * v + 128], T.shb[:, :], True, True))
+    wt(V, "pb")
+    for t in range(2):
+        tsc("ohc", T.oh[:, 256 * t:256 * t + 256], T.pb1[:, 0:256], T.kcol[:, t:t + 1], OP.is_equal)
+    wt(V, "dr")
+    sg("tr", V.transpose(T.tt[:, 0:64], T.ts[:, 0:64]))
+    wt(V, "tr")
+    sg("tab", V.tensor_copy(T.tabr[:, :], T.tt[:, 0:64]))
+
+    def lookup(sem, ps, at, oh, tab):
+        for q in range(2):
+            for t in range(2):
+                sg(sem, TE.matmul(ps[:, at + 32 * q:at + 32 * q + 32], oh[:, 256 * t + 128 * q:256 * t + 128 * q + 128],
+                                  tab[:, 32 * t:32 * t + 32], t == 0, t == 1))
+    wt(TE, "ohc", "tab")
+    lookup("pA", T.psa, 0, T.oh, T.tabr)
+
+    plan = {rk: calls(rank, rk, T, topo) for rk in RK}
+    order = {rk: [x for call in plan[rk] for x in call] for rk in RK}
+    slot_order = [x[0] for x in order[(0, 0)]]
+    wt(V, "pS", "c4")
+    hm = M // 2
+    for i, p in enumerate(slot_order):
+        tsc("vl0", T.l0[:, hm * i:hm * i + hm], T.cw[:, :], T.pss[:, 4 * (p % 2) + p // 2:4 * (p % 2) + p // 2 + 1], OP.add)
+    wt(V, "pA")
+    for q in range(2):
+        tsc("vlf", T.lf0[:, q:48:2], T.psa[:, 32 * q:32 * q + 24], T.i24[:, q:q + 1], OP.add)
+
+    H = OWN // 2
+
+    def gathers(r, k, win, lf, need):
+        tag = "%d%d" % (r, k)
+        w, s, c0 = T["w" + tag], T["s" + tag], 2 * M * k
+        if need:
+            wt(V, *need)
+            wt(S, *need)
+        sg("f" + tag, V.tensor_copy(w[:, 0:H], win[:, :].indirect(lf[:, c0:c0 + M])))
+        sg("f" + tag, S.activation(w[:, H:OWN], win[:, :].indirect(lf[:, c0 + M:c0 + 2 * M]), AF.Copy))
+        wt(V, "f" + tag)
+        wt(S, "f" + tag)
+        sg("s" + tag, V.tensor_copy(s[:, 0:3 * REG], w[:, 0:OWN].indirect(T.l0[:, 0:3 * hm])))
+        sg("s" + tag, S.activation(s[:, 3 * REG:6 * REG], w[:, 0:OWN].indirect(T.l0[:, 3 * hm:6 * hm]), AF.Copy))
+        last = w[:, 0:OWN].indirect(T.l0[:, 6 * hm:7 * hm])
+        if k == 0:
+            sg("t" + tag, V.tensor_copy(s[:, 6 * REG:7 * REG], last))
+        else:
+            sg("t" + tag, S.activation(s[:, 6 * REG:7 * REG], last, AF.Copy))
+
+    def send(r, k):
+        tag, at = "%d%d" % (r, k), OWN + REG * rank
+        relayed = routes(rank, (r, k), T, topo)[1]
+        for call in plan[(r, k)]:
+            wt(g, ("t" if topo.chip(call[0][1]) == topo.chip(core) and call[0][0] not in relayed else "s") + tag)
+            tr = []
+            for p, c, e in call:
+                i = slot_order.index(p)
+                src = T["s" + tag][:, REG * i:REG * i + REG]
+                if p in relayed:
+                    j = relayed.index(p)
+                    tr.append(transfer(topo, c, T["rl" + tag][:, REG * j:REG * j + REG], src, T.sem["rel" + tag], e))
+                else:
+                    tr.append(transfer(topo, c, T["w" + tag][:, at:at + REG], src, T.sem["arr" + tag], e))
+                cnt["lsem"] = cnt.get("lsem", 0) + len(e)
+            g.remote_dma_fused(tr, local_sem=T.sem["lsem"])
+
+    def arrivals(r, k):
+        n = 0
+        for src in range(NR):
+            if src != rank:
+                n += sum(len(e) for call in calls(src, (r, k), T, topo) for p, c, e in call if p == rank and c == core)
+                n += sum(len(e) for p, e in hand_on(src, (r, k), T, topo) if p == rank)
+        return n
+
+    def maxima(r, k, out):
+        tag = "%d%d" % (r, k)
+        w, sq = T["w" + tag], T["q" + tag]
+        n = arrivals(r, k)
+        V.wait_ge(T.sem["arr" + tag], n)
+        S.wait_ge(T.sem["arr" + tag], n)
+        for h, s in enumerate(("na", "nb")):
+            sg(s + tag, S.activation(sq[:, H * h:H * h + H], w[:, :].indirect(T.ln[:, M * h:M * h + M]), AF.Copy))
+        for n in range(1, 6):
+            for h, (s, a) in enumerate((("na", "aa"), ("nb", "ab"))):
+                dst = out[:, OWN * k + H * h:OWN * k + H * h + H]
+                wt(V, (s if n == 1 else a) + tag)
+                ttn(a + tag, dst, w[:, :].indirect(T.ln[:, 2 * M * n + M * h:2 * M * n + M * h + M]),
+                    sq[:, H * h:H * h + H] if n == 1 else dst, OP.max)
+
+    gathers(0, 0, T.xs, T.lf0, ("vlf", "dx", "vl0"))
+    gathers(0, 1, T.xs, T.lf0, ())
+    send(0, 0)
+    send(0, 1)
+
+    for r, k in RK:
+        at = OWN + REG * rank
+        sg("vown", V.memset(T["w%d%d" % (r, k)][:, at:at + REG], 0.0))
+    wt(V, "dm")
+    tsc("b1", T.hi[:, :], T.nb[:, :], 3, OP.arith_shift_right)
+    tsc("b1", T.lo[:, :], T.nb[:, :], 7, OP.bitwise_and)
+    tsc("b1", T.own[:, :], T.nb[:, :], 32.0, OP.is_lt)
+    sg("afc", V.tensor_copy(T.actf[:, :], T.acti[:, :]))
+    sg("afc", V.tensor_copy(T.posf[:, :], T.posi[:, :]))
+    wt(V, "dc", "b1")
+    tsc("b2", T.sb0[:, :], T.hi[:, :], float(REG), OP.mult)
+    tsc("b2", T.st[:, :], T.own[:, :], 24.0, OP.mult, 8.0, OP.add)
+    sg("ctr", V.transpose(T.tt[:, 64:128], T.ts[:, 64:128]))
+    sg("ctb", V.tensor_copy(T.tabc[:, :], T.ts[:, 64:128]))
+    wt(V, "b2")
+    ttn("b3", T.sb1[:, :], T.sb0[:, :], T.lo[:, :], OP.add)
+    wt(V, "ctr")
+    sg("ctb", V.tensor_copy(T.tabt[:, :], T.tt[:, 64:128]))
+    wt(TE, "ctb")
+    lookup("pB", T.psb, 0, T.oh, T.tabc)
+    wt(V, "b3", "i4")
+    ttn("b4", T.df[:, :], T.nb[:, :], T.sb1[:, :], OP.subtract)
+    tsc("c5", T.idb[:, :], T.idf[:, :], 0.0, OP.is_equal)
+    wt(V, "b4", "afc")
+    ttn("b5", T.dg[:, :], T.df[:, :], T.own[:, :], OP.mult)
+    for q in range(2):
+        tsc("m1", T.mk[:, 32 * q:32 * q + 24], T.u24[:, :], T.actf[:, q:q + 1], OP.is_equal)
+    wt(V, "b5")
+    ttn("b6", T.base[:, :], T.dg[:, :], T.sb1[:, :], OP.add)
+    wt(V, "m1", "pB")
+    for q in range(2):
+        ttn("m2", T.mx[:, 32 * q:32 * q + 24], T.mk[:, 32 * q:32 * q + 24], T.psb[:, 32 * q:32 * q + 24], OP.mult)
+    wt(V, "b6")
+    for n in range(6):
+        for q in range(2):
+            j = 2 * n + q
+            tsc("b7", T.ln[:, 2 * M * n + q:2 * M * n + 2 * M:2], T.u24[:, 0:M], T.st[:, j:j + 1], OP.mult, T.base[:, j:j + 1], OP.add)
+
+    def spread(src, enc, dg, s_in, s_enc, s_dg, pb, s_pb, oh, s_oh):
+        wt(V, s_in)
+        tsc(s_enc, enc[:, :], src[:, :], T.g32[:, 0:1], OP.add)
+        wt(V, s_enc, "c5")
+        for q in range(2):
+            tsc(s_dg, dg[:, 128 * q:128 * q + 128], T.idb[:, :], enc[:, q:q + 1], OP.mult)
+        wt(TE, s_dg)
+        sg(s_pb, TE.matmul(pb[:, 0:256], T.ones[:, :], dg[:, :], True, True))
+        wt(V, s_pb)
+        for t in range(2):
+            tsc(s_oh, oh[:, 256 * t:256 * t + 256], pb[:, 0:256], T.kcol[:, t:t + 1], OP.is_equal)
+        wt(TE, s_oh)
+    wt(V, "m2")
+    for q in range(2):
+        sg("m3", V.tensor_reduce(T.a1[:, q:q + 1], T.mx[:, 32 * q:32 * q + 24], AxisListType.X, OP.add))
+    spread(T.a1, T.a1e, T.dg2, "m3", "m4", "d2", T.pb2, "p2", T.oh2, "o2")
+    lookup("pC", T.psc, 64, T.oh2, T.tabt)
+    lookup("pC", T.psc, 0, T.oh2, T.tabc)
+    wt(V, "pC")
+    for q in range(2):
+        tsc("e1", T.mk2[:, 32 * q:32 * q + 24], T.psc[:, 64 + 32 * q:64 + 32 * q + 24], T.posf[:, q:q + 1], OP.is_equal)
+    for q in range(2):
+        tsc("vly", T.ly[:, q:48:2], T.psc[:, 32 * q:32 * q + 24], 32.0, OP.mult, T.r16[:, q:q + 1], OP.add)
+    wt(V, "e1")
+    for q in range(2):
+        ttn("e2", T.mx2[:, 32 * q:32 * q + 24], T.mk2[:, 32 * q:32 * q + 24], T.u24[:, :], OP.mult)
+    wt(V, "e2")
+    for q in range(2):
+        sg("e3", V.tensor_reduce(T.k1[:, q:q + 1], T.mx2[:, 32 * q:32 * q + 24], AxisListType.X, OP.add))
+    spread(T.k1, T.k1e, T.dg3, "e3", "e4", "d3", T.pb3, "p3", T.oh3, "o3")
+    lookup("pD", T.psd, 0, T.oh3, T.tabc)
+    wt(V, "i5")
+    tsc("j1", T.jj[:, :], T.jt[:, :], T.g16[:, 0:1], OP.subtract)
+    wt(V, "j1")
+    tsc("j2", T.jm[:, :], T.jj[:, :], 2731.0, OP.mult)
+    tsc("j2", T.jb[:, :], T.jj[:, :], 32.0, OP.mult)
+    wt(V, "j2")
+    tsc("j3", T.ji[:, :], T.jm[:, :], 16, OP.arith_shift_right)
+    wt(V, "pD")
+    for q in range(2):
+        tsc("vl1", T.lf1[:, q:48:2], T.psd[:, 32 * q:32 * q + 24], 32.0, OP.mult, T.r16[:, q:q + 1], OP.add)
+    wt(V, "j3")
+    tsc("j4", T.ja[:, :], T.ji[:, :], -767.0, OP.mult)
+    wt(V, "j4")
+    ttn("j5", T.jc[:, :], T.ja[:, :], T.jb[:, :], OP.add)
+    wt(V, "j5")
+    sg("j5", V.tensor_copy(T.lc[:, :], T.jc[:, :]))
+
+    wt(V, "b7", "vown")
+    wt(S, "b7", "vown")
+    for k in range(CH):
+        maxima(0, k, T.n0)
+    gathers(1, 0, T.n0, T.lf1, ("aa00", "ab00", "aa01", "ab01", "vl1"))
+    gathers(1, 1, T.n0, T.lf1, ())
+    send(1, 0)
+    send(1, 1)
+    for k in range(CH):
+        maxima(1, k, T.n1)
+
+    need = ("aa10", "ab10", "aa11", "ab11", "vly", "j5")
+    wt(V, *need)
+    wt(S, *need)
+    sg("y1", V.tensor_copy(T.yp[:, 0:384], T.n1[:, :].indirect(T.ly[:, 0:24])))
+    sg("y1", S.activation(T.yp[:, 384:768], T.n1[:, :].indirect(T.ly[:, 24:48]), AF.Copy))
+    wt(V, "y1")
+    wt(S, "y1")
+    sg("y2a", V.tensor_copy(T.ys[:, 0:384], T.yp[:, :].indirect(T.lc[:, 0:24])))
+    sg("y2b", S.activation(T.ys[:, 384:768], T.yp[:, :].indirect(T.lc[:, 24:48]), AF.Copy))
+    wt(Y, "y2a")
+    sg("dy", Y.dma_start(T.y[:, 0:384], T.ys[:, 0:384]), 16)
+    wt(S, "y2b")
+    sg("dy", S.dma_start(T.y[:, 384:768], T.ys[:, 384:768]), 16)
+    for name in cnt:
+        if seen.get(name, 0) < cnt[name]:
+            wt(g, name)

@@ -1,11 +1,12 @@
 from concourse.bass import DstId, RemoteDMATransfer
-from concourse.mybir import AluOpType as OP, AxisListType, ActivationFunctionType as AF
+from concourse.mybir import AluOpType as OP, ActivationFunctionType as AF
 
-NR, CH, M = 8, 2, 12
+NR, M = 8, 12
+CH = 24 // M
 OWN, REG = 32 * M, 8 * M
 WIN = OWN + NR * REG
 RK = [(r, k) for r in range(2) for k in range(CH)]
-RELAY = {(0, 0): True, (0, 1): True, (1, 0): True, (1, 1): True}
+RELAY = {rk: True for rk in RK}
 
 F32, I32, U16, B16 = "float32", "int32", "uint16", "bfloat16"
 SCRATCH = {
@@ -14,40 +15,37 @@ SCRATCH = {
     "ts": ("sbuf", [128, 128], I32), "tt": ("sbuf", [128, 128], I32), "tabr": ("sbuf", [128, 64], B16),
     "tabc": ("sbuf", [128, 64], B16), "tabt": ("sbuf", [128, 64], B16),
     "prow": ("sbuf", [128, 256], I32), "rowe": ("sbuf", [128, 256], B16),
-    "shi": ("sbuf", [128, 4], I32), "shb": ("sbuf", [128, 4], B16),
+    "shi": ("sbuf", [128, 4], I32), "shf": ("sbuf", [128, 4], F32), "shx": ("sbuf", [128, 2 * M], B16),
     "nb": ("sbuf", [128, 12], I32), "acti": ("sbuf", [128, 2], I32), "posi": ("sbuf", [128, 2], I32),
     "actf": ("sbuf", [128, 2], F32), "posf": ("sbuf", [128, 2], F32),
-    "ones": ("sbuf", [128, 128], B16), "idf": ("sbuf", [128, 128], F32), "idb": ("sbuf", [128, 128], B16),
+    "ones": ("sbuf", [128, 128], B16), "idb": ("sbuf", [128, 128], B16),
     "rt": ("sbuf", [128, 128], F32), "rp": ("sbuf", [128, 256], B16),
-    "pidx": ("sbuf", [128, 2], I32), "ri": ("sbuf", [128, 2], I32), "wi": ("sbuf", [128, 2], I32), "gi": ("sbuf", [128, 2], I32),
-    "i24": ("sbuf", [128, 2], F32), "r16": ("sbuf", [128, 2], F32), "w32": ("sbuf", [128, 2], F32), "g32": ("sbuf", [128, 2], F32),
-    "g16": ("sbuf", [128, 2], F32),
-    "kcol": ("sbuf", [128, 2], F32), "rc": ("sbuf", [128, 256], F32), "cwi": ("sbuf", [128, M // 2], F32), "cw": ("sbuf", [128, M // 2], F32),
-    "u24": ("sbuf", [128, 24], F32), "jt": ("sbuf", [128, 48], I32), "jj": ("sbuf", [128, 48], I32), "jm": ("sbuf", [128, 48], I32),
-    "ji": ("sbuf", [128, 48], I32), "ja": ("sbuf", [128, 48], F32), "jb": ("sbuf", [128, 48], F32), "jc": ("sbuf", [128, 48], F32),
+    "pidx": ("sbuf", [128, 2], I32), "ri": ("sbuf", [128, 2], I32), "wi": ("sbuf", [128, 2], I32),
+    "i24": ("sbuf", [128, 2], F32), "r16": ("sbuf", [128, 2], F32), "w32": ("sbuf", [128, 2], F32), "lcs": ("sbuf", [128, 4], F32),
+    "kcol": ("sbuf", [128, 2], F32), "rcb": ("sbuf", [128, 256], B16), "cwi": ("sbuf", [128, 4 * M], F32), "cwb": ("sbuf", [128, 4 * M], B16),
+    "u48": ("sbuf", [128, 48], F32), "m2i": ("sbuf", [128, 16], F32),
     "lc": ("sbuf", [128, 48], U16), "lf0": ("sbuf", [128, 48], U16), "lf1": ("sbuf", [128, 48], U16), "ly": ("sbuf", [128, 48], U16),
-    "l0": ("sbuf", [128, 7 * (M // 2) + 6], U16), "ln": ("sbuf", [128, 6 * 2 * M], U16),
+    "l0": ("sbuf", [128, 4 * M], U16), "ln": ("sbuf", [128, 12 * M], U16), "lnf": ("sbuf", [128, 12 * M], F32),
     "oh": ("sbuf", [128, 512], B16), "oh2": ("sbuf", [128, 512], B16), "oh3": ("sbuf", [128, 512], B16),
     "dg2": ("sbuf", [128, 256], B16), "dg3": ("sbuf", [128, 256], B16),
-    "hi": ("sbuf", [128, 12], I32), "lo": ("sbuf", [128, 12], I32), "own": ("sbuf", [128, 12], F32), "st": ("sbuf", [128, 12], F32),
-    "sb0": ("sbuf", [128, 12], F32), "sb1": ("sbuf", [128, 12], F32), "df": ("sbuf", [128, 12], F32), "dg": ("sbuf", [128, 12], F32),
-    "base": ("sbuf", [128, 12], F32),
-    "mk": ("sbuf", [128, 64], F32), "mx": ("sbuf", [128, 64], F32), "a1": ("sbuf", [128, 2], F32), "a1e": ("sbuf", [128, 2], F32),
-    "mk2": ("sbuf", [128, 64], F32), "mx2": ("sbuf", [128, 64], F32), "k1": ("sbuf", [128, 2], F32), "k1e": ("sbuf", [128, 2], F32),
+    "hi": ("sbuf", [128, 12], I32), "m88": ("sbuf", [128, 12], F32), "st0": ("sbuf", [128, 12], F32), "st": ("sbuf", [128, 12], F32),
+    "hm": ("sbuf", [128, 12], F32), "base": ("sbuf", [128, 12], F32),
+    "mk": ("sbuf", [128, 48], F32), "mx": ("sbuf", [128, 48], F32), "my": ("sbuf", [128, 48], F32), "a1": ("sbuf", [128, 2], F32),
+    "mk2": ("sbuf", [128, 48], F32), "mx2": ("sbuf", [128, 48], F32), "my2": ("sbuf", [128, 48], F32), "k1": ("sbuf", [128, 2], F32),
 }
 for _n in ("pb1", "psa", "psb", "pss", "pb2", "psc", "pb3", "psd"):
     SCRATCH[_n] = ("psum", [128, 512], F32)
 for _r, _k in RK:
     SCRATCH["w%d%d" % (_r, _k)] = ("sbuf", [128, WIN], F32)
-    SCRATCH["s%d%d" % (_r, _k)] = ("sbuf", [128, 7 * REG], F32)
+    SCRATCH["s%d%d" % (_r, _k)] = ("sbuf", [128, 8 * REG], F32)
     SCRATCH["q%d%d" % (_r, _k)] = ("sbuf", [128, OWN], F32)
     SCRATCH["rl%d%d" % (_r, _k)] = ("sbuf", [128, 2 * REG], F32)
-SEMAPHORES = ["ms", "one", "vown", "i1", "i2", "i3", "i4", "i5", "c1", "c2", "c3", "c4", "c5", "j1", "j2", "j3", "j4", "j5",
-              "dp", "ds", "dr", "dx", "dc", "dm", "dy", "row", "pb", "shc", "pS", "tr", "tab", "ohc", "pA", "pB", "vl0", "vlf",
-              "ctr", "ctb", "afc", "m1", "m2", "m3", "m4", "d2", "p2", "o2", "pC", "vly", "e1", "e2", "e3", "e4", "d3", "p3", "o3", "pD", "vl1",
-              "b1", "b2", "b3", "b4", "b5", "b6", "b7", "y1", "y2a", "y2b", "lsem"]
+SEMAPHORES = ["ms", "one", "vown", "i1", "i2", "i3", "i4", "i5", "i6", "i7", "c1", "c2", "c3", "c4", "c6", "j5",
+              "dp", "ds", "dr", "dx", "dc", "da", "dn", "dy", "row", "pb", "shc", "shx", "pS", "tr", "tab", "ohc", "pA", "pB", "vl0", "vlf",
+              "ctr", "ctb", "afc", "m1", "m2", "m3", "d2", "p2", "o2", "pC", "vly", "e1", "e2", "e3", "d3", "p3", "o3", "pD", "vl1",
+              "b1", "b2", "b3", "b6", "b7", "y1", "y2a", "y2b", "lsem"]
 for _r, _k in RK:
-    SEMAPHORES += [_s + "%d%d" % (_r, _k) for _s in ("f", "s", "t", "arr", "rel", "na", "nb", "aa", "ab")]
+    SEMAPHORES += [_s + "%d%d" % (_r, _k) for _s in ("f", "s", "arr", "rel", "na", "nb", "aa", "ab")]
 
 
 def routes(src, rk, T, topo):
@@ -159,14 +157,13 @@ def rank_program(g, core, T, topo):
         for gg in range(4):
             q = Y if gg < 2 else S
             sg("dr", q.dma_start(T.ts[32 * gg:32 * gg + 24, 32 * t:32 * t + 24], T.rel[4 * t + gg:4 * t + gg + 1, :]), 16)
-    sg("dx", Y.dma_start(T.xs[:, :], T.x[:, :]), 16)
+    sg("dx", S.dma_start(T.xs[:, :], T.x[:, :]), 16)
+    sg("da", S.dma_start(T.posi[:, :], T.pose[:, :]), 16)
+    sg("da", Y.dma_start(T.acti[:, :], T.act[:, :]), 16)
     for t in range(2):
         for gg in range(4):
-            q = Y if gg < 2 else S
-            sg("dc", q.dma_start(T.ts[32 * gg:32 * gg + 24, 64 + 32 * t:64 + 32 * t + 24], T.ct[4 * t + gg:4 * t + gg + 1, :]), 16)
-    sg("dm", S.dma_start(T.nb[:, :], T.nbr[:, :]), 16)
-    sg("dm", S.dma_start(T.acti[:, :], T.act[:, :]), 16)
-    sg("dm", S.dma_start(T.posi[:, :], T.pose[:, :]), 16)
+            sg("dc", Y.dma_start(T.ts[32 * gg:32 * gg + 24, 64 + 32 * t:64 + 32 * t + 24], T.ct[4 * t + gg:4 * t + gg + 1, :]), 16)
+    sg("dn", Y.dma_start(T.nb[:, :], T.nbr[:, :]), 16)
 
     def iota(sem, out, pattern, cm, flag=True):
         if flag:
@@ -175,96 +172,105 @@ def rank_program(g, core, T, topo):
             sg(sem, g.iota(out, pattern, 0, cm))
     iota("i1", T.pidx[:, 0:1], [[0, 1]], 1, False)
     iota("i2", T.rt[:, :], [[-16, 8], [0, 2], [-1, 8]], 1)
-    iota("i3", T.cwi[:, :], [[64, M // 2]], 0)
-    iota("i3", T.rc[0:1, :], [[0, 2], [32, 8], [0, 16]], 0)
-    iota("i3", T.kcol[:, :], [[128, 2]], 1)
-    iota("i4", T.u24[:, :], [[1, 24]], 0)
-    iota("i4", T.idf[:, :], [[-1, 128]], 1)
-    iota("i5", T.jt[:, :], [[16, 48]], 1, False)
+    iota("i3", T.rcb[0:1, :], [[0, 2], [32, 8], [0, 16]], 0)
+    iota("i4", T.cwi[:, :], [[0, 8], [64, M // 2]], 0)
+    iota("i5", T.kcol[:, :], [[128, 2]], 1)
+    wt(g, "one")
+    sg("i6", g.affine_select(T.idb[:, :], T.ones[:, :], [[-1, 128]], OP.is_equal, 0.0, 0, 1))
+    iota("i7", T.u48[:, :], [[0, 2], [1, 24]], 0)
+    iota("i7", T.m2i[:, :], [[2, 16]], 0)
+    for r, k in RK:
+        at = OWN + REG * rank
+        iota("vown", T["w%d%d" % (r, k)][:, at:at + REG], [[0, REG]], 0)
 
     wt(V, "i1")
     p1 = T.pidx[:, 0:1]
     tsc("c1", T.ri[:, 0:1], p1, 15, OP.bitwise_and)
     tsc("c1", T.wi[:, 0:1], p1, 3, OP.arith_shift_right, 1, OP.bitwise_and)
-    tsc("c1", T.gi[:, 0:1], p1, 4, OP.arith_shift_right)
     wt(V, "i2")
     for v in range(2):
         tsc("c3", T.rp[:, 128 * v:128 * v + 128], T.rt[:, :], 8.0 * v, OP.is_equal)
     wt(V, "c1")
+    tsc("c2", T.w32[:, 0:1], T.wi[:, 0:1], 32.0, OP.mult)
     for q in range(2):
         tsc("c2", T.i24[:, q:q + 1], T.ri[:, 0:1], 24.0, OP.mult, 384.0 * q, OP.add)
-        tsc("c2", T.r16[:, q:q + 1], T.ri[:, 0:1], 16.0 * q, OP.add)
-    tsc("c2", T.w32[:, 0:1], T.wi[:, 0:1], 32.0, OP.mult)
-    tsc("c2", T.g32[:, 0:1], T.gi[:, 0:1], 32.0, OP.mult)
-    tsc("c2", T.g16[:, 0:1], T.gi[:, 0:1], 16.0, OP.mult)
-    wt(V, "i3", "c2")
-    tsc("c4", T.cw[:, :], T.cwi[:, :], T.w32[:, 0:1], OP.add)
+    wt(V, "i4", "c2")
+    tsc("c4", T.cwb[:, :], T.cwi[:, :], T.w32[:, 0:1], OP.add)
 
+    wt(V, "ds")
+    sg("shc", V.tensor_copy(T.shf[:, :], T.shi[:, :]))
+    wt(S, "shc", "one")
+    hm = M // 2
+    for j in range(4):
+        sg("shx", S.activation(T.shx[:, j * hm:j * hm + hm], T.ones[:, 0:hm], AF.Copy, scale=T.shf[:, j:j + 1]))
     wt(V, "dp")
     for q in range(2):
-        ttn("row", T.rowe[0:1, 128 * q:128 * q + 128], T.prow[0:1, q:256:2], T.rc[0:1, 128 * q:128 * q + 128], OP.add)
-    wt(TE, "row", "one")
-    sg("pb", TE.matmul(T.pb1[:, 0:256], T.ones[0:1, 0:128], T.rowe[0:1, 0:256], True, True))
-    wt(V, "ds")
-    sg("shc", V.tensor_copy(T.shb[:, :], T.shi[:, :]))
-    wt(TE, "shc", "c3")
-    for v in range(2):
-        sg("pS", TE.matmul(T.pss[:, 4 * v:4 * v + 4], T.rp[:, 128 * v:128 * v + 128], T.shb[:, :], True, True))
-    wt(V, "pb")
-    for t in range(2):
-        tsc("ohc", T.oh[:, 256 * t:256 * t + 256], T.pb1[:, 0:256], T.kcol[:, t:t + 1], OP.is_equal)
-    wt(V, "dr")
-    sg("tr", V.transpose(T.tt[:, 0:64], T.ts[:, 0:64]))
-    wt(V, "tr")
-    sg("tab", V.tensor_copy(T.tabr[:, :], T.tt[:, 0:64]))
+        sg("row", V.tensor_copy(T.rowe[0:1, 128 * q:128 * q + 128], T.prow[0:1, q:256:2]))
+
+    def all_rows(sem, pb, lhs, rhs):
+        sg(sem, TE.matmul(pb[:, 0:256], T.ones[0:1, :], T.rcb[0:1, :], True, False))
+        sg(sem, TE.matmul(pb[:, 0:256], lhs, rhs, False, True))
+
+    def compare(pb, s_pb, oh, s_oh):
+        wt(V, s_pb)
+        for t in range(2):
+            tsc(s_oh, oh[:, 256 * t:256 * t + 256], pb[:, 0:256], T.kcol[:, t:t + 1], OP.is_equal)
 
     def lookup(sem, ps, at, oh, tab):
         for q in range(2):
             for t in range(2):
-                sg(sem, TE.matmul(ps[:, at + 32 * q:at + 32 * q + 32], oh[:, 256 * t + 128 * q:256 * t + 128 * q + 128],
-                                  tab[:, 32 * t:32 * t + 32], t == 0, t == 1))
-    wt(TE, "ohc", "tab")
+                sg(sem, TE.matmul(ps[:, at + 24 * q:at + 24 * q + 24], oh[:, 256 * t + 128 * q:256 * t + 128 * q + 128],
+                                  tab[:, 32 * t:32 * t + 24], t == 0, t == 1))
+    wt(TE, "one", "i3", "row")
+    all_rows("pb", T.pb1, T.ones[0:1, :], T.rowe[0:1, :])
+    wt(TE, "shx", "c3", "i6", "c4")
+    for v in range(2):
+        o = T.pss[:, 2 * M * v:2 * M * v + 2 * M]
+        sg("pS", TE.matmul(o, T.rp[:, 128 * v:128 * v + 128], T.shx[:, :], True, False))
+        sg("pS", TE.matmul(o, T.idb[:, :], T.cwb[:, 2 * M * v:2 * M * v + 2 * M], False, True))
+    wt(V, "dr")
+    sg("tr", V.transpose(T.tt[:, 0:64], T.ts[:, 0:64]))
+    wt(V, "i5")
+    wt(V, "tr")
+    sg("tab", V.tensor_copy(T.tabr[:, :], T.tt[:, 0:64]))
+    compare(T.pb1, "pb", T.oh, "ohc")
+    wt(TE, "tab", "ohc")
     lookup("pA", T.psa, 0, T.oh, T.tabr)
-
-    plan = {rk: calls(rank, rk, T, topo) for rk in RK}
-    order = {rk: [x for call in plan[rk] for x in call] for rk in RK}
-    slot_order = [x[0] for x in order[(0, 0)]]
-    wt(V, "pS", "c4")
-    hm = M // 2
-    for i, p in enumerate(slot_order):
-        tsc("vl0", T.l0[:, hm * i:hm * i + hm], T.cw[:, :], T.pss[:, 4 * (p % 2) + p // 2:4 * (p % 2) + p // 2 + 1], OP.add)
+    wt(V, "pS")
+    sg("vl0", V.tensor_copy(T.l0[:, :], T.pss[:, 0:4 * M]))
+    wt(V, "dc")
+    sg("ctb", V.tensor_copy(T.tabc[:, :], T.ts[:, 64:128]))
+    wt(TE, "ctb")
+    lookup("pB", T.psb, 0, T.oh, T.tabc)
     wt(V, "pA")
     for q in range(2):
-        tsc("vlf", T.lf0[:, q:48:2], T.psa[:, 32 * q:32 * q + 24], T.i24[:, q:q + 1], OP.add)
+        tsc("vlf", T.lf0[:, q:48:2], T.psa[:, 24 * q:24 * q + 24], T.i24[:, q:q + 1], OP.add)
 
     H = OWN // 2
+    plan = {rk: calls(rank, rk, T, topo) for rk in RK}
 
-    def gathers(r, k, win, lf, need):
-        tag = "%d%d" % (r, k)
-        w, s, c0 = T["w" + tag], T["s" + tag], 2 * M * k
-        if need:
-            wt(V, *need)
-            wt(S, *need)
+    def own_chunk(r, k, win, lf):
+        tag, c0 = "%d%d" % (r, k), 2 * M * k
+        w = T["w" + tag]
         sg("f" + tag, V.tensor_copy(w[:, 0:H], win[:, :].indirect(lf[:, c0:c0 + M])))
         sg("f" + tag, S.activation(w[:, H:OWN], win[:, :].indirect(lf[:, c0 + M:c0 + 2 * M]), AF.Copy))
+
+    def slots(r, k):
+        tag = "%d%d" % (r, k)
+        w, s = T["w" + tag], T["s" + tag]
         wt(V, "f" + tag)
         wt(S, "f" + tag)
-        sg("s" + tag, V.tensor_copy(s[:, 0:3 * REG], w[:, 0:OWN].indirect(T.l0[:, 0:3 * hm])))
-        sg("s" + tag, S.activation(s[:, 3 * REG:6 * REG], w[:, 0:OWN].indirect(T.l0[:, 3 * hm:6 * hm]), AF.Copy))
-        last = w[:, 0:OWN].indirect(T.l0[:, 6 * hm:7 * hm])
-        if k == 0:
-            sg("t" + tag, V.tensor_copy(s[:, 6 * REG:7 * REG], last))
-        else:
-            sg("t" + tag, S.activation(s[:, 6 * REG:7 * REG], last, AF.Copy))
+        sg("s" + tag, V.tensor_copy(s[:, 0:4 * REG], w[:, 0:OWN].indirect(T.l0[:, 0:4 * hm])))
+        sg("s" + tag, S.activation(s[:, 4 * REG:8 * REG], w[:, 0:OWN].indirect(T.l0[:, 4 * hm:8 * hm]), AF.Copy))
 
     def send(r, k):
         tag, at = "%d%d" % (r, k), OWN + REG * rank
         relayed = routes(rank, (r, k), T, topo)[1]
+        wt(g, "s" + tag)
         for call in plan[(r, k)]:
-            wt(g, ("t" if topo.chip(call[0][1]) == topo.chip(core) and call[0][0] not in relayed else "s") + tag)
             tr = []
             for p, c, e in call:
-                i = slot_order.index(p)
+                i = 4 * (p % 2) + p // 2
                 src = T["s" + tag][:, REG * i:REG * i + REG]
                 if p in relayed:
                     j = relayed.index(p)
@@ -297,109 +303,102 @@ def rank_program(g, core, T, topo):
                 ttn(a + tag, dst, w[:, :].indirect(T.ln[:, 2 * M * n + M * h:2 * M * n + M * h + M]),
                     sq[:, H * h:H * h + H] if n == 1 else dst, OP.max)
 
-    gathers(0, 0, T.xs, T.lf0, ("vlf", "dx", "vl0"))
-    gathers(0, 1, T.xs, T.lf0, ())
-    send(0, 0)
-    send(0, 1)
-
-    for r, k in RK:
-        at = OWN + REG * rank
-        sg("vown", V.memset(T["w%d%d" % (r, k)][:, at:at + REG], 0.0))
-    wt(V, "dm")
-    tsc("b1", T.hi[:, :], T.nb[:, :], 3, OP.arith_shift_right)
-    tsc("b1", T.lo[:, :], T.nb[:, :], 7, OP.bitwise_and)
-    tsc("b1", T.own[:, :], T.nb[:, :], 32.0, OP.is_lt)
+    wt(V, "vlf", "dx", "vl0")
+    wt(S, "vlf", "dx", "vl0")
+    own_chunk(0, 0, T.xs, T.lf0)
+    slots(0, 0)
+    for k in range(1, CH):
+        own_chunk(0, k, T.xs, T.lf0)
+    wt(V, "da")
     sg("afc", V.tensor_copy(T.actf[:, :], T.acti[:, :]))
     sg("afc", V.tensor_copy(T.posf[:, :], T.posi[:, :]))
-    wt(V, "dc", "b1")
-    tsc("b2", T.sb0[:, :], T.hi[:, :], float(REG), OP.mult)
-    tsc("b2", T.st[:, :], T.own[:, :], 24.0, OP.mult, 8.0, OP.add)
-    sg("ctr", V.transpose(T.tt[:, 64:128], T.ts[:, 64:128]))
-    sg("ctb", V.tensor_copy(T.tabc[:, :], T.ts[:, 64:128]))
-    wt(V, "b2")
-    ttn("b3", T.sb1[:, :], T.sb0[:, :], T.lo[:, :], OP.add)
-    wt(V, "ctr")
-    sg("ctb", V.tensor_copy(T.tabt[:, :], T.tt[:, 64:128]))
-    wt(TE, "ctb")
-    lookup("pB", T.psb, 0, T.oh, T.tabc)
-    wt(V, "b3", "i4")
-    ttn("b4", T.df[:, :], T.nb[:, :], T.sb1[:, :], OP.subtract)
-    tsc("c5", T.idb[:, :], T.idf[:, :], 0.0, OP.is_equal)
-    wt(V, "b4", "afc")
-    ttn("b5", T.dg[:, :], T.df[:, :], T.own[:, :], OP.mult)
+    for k in range(1, CH):
+        slots(0, k)
+    for k in range(CH):
+        send(0, k)
+
+    wt(V, "afc", "i7")
     for q in range(2):
-        tsc("m1", T.mk[:, 32 * q:32 * q + 24], T.u24[:, :], T.actf[:, q:q + 1], OP.is_equal)
-    wt(V, "b5")
-    ttn("b6", T.base[:, :], T.dg[:, :], T.sb1[:, :], OP.add)
+        tsc("m1", T.mk[:, 24 * q:24 * q + 24], T.u48[:, 0:24], T.actf[:, q:q + 1], OP.is_equal)
     wt(V, "m1", "pB")
-    for q in range(2):
-        ttn("m2", T.mx[:, 32 * q:32 * q + 24], T.mk[:, 32 * q:32 * q + 24], T.psb[:, 32 * q:32 * q + 24], OP.mult)
-    wt(V, "b6")
+    ttn("m2", T.mx[:, :], T.mk[:, :], T.psb[:, 0:48], OP.mult)
+
+    def spread(mx, my, num, dg, s_in, s_num, s_dg, pb, s_pb):
+        wt(S, s_in)
+        for q in range(2):
+            c = slice(24 * q, 24 * q + 24)
+            sg(s_num, S.activation(my[:, c], mx[:, c], AF.Copy, accum_out=num[:, q:q + 1]))
+        wt(S, s_num, "i6")
+        for q in range(2):
+            sg(s_dg, S.activation(dg[:, 128 * q:128 * q + 128], T.idb[:, :], AF.Copy, scale=num[:, q:q + 1]))
+        wt(TE, s_dg)
+        all_rows(s_pb, pb, T.ones[:, :], dg[:, :])
+    spread(T.mx, T.my, T.a1, T.dg2, "m2", "m3", "d2", T.pb2, "p2")
+    wt(V, "dn")
+    tsc("b1", T.hi[:, :], T.nb[:, :], 3, OP.arith_shift_right)
+    tsc("b1", T.m88[:, :], T.nb[:, :], 32.0, OP.is_ge, float(REG - 8), OP.mult)
+    tsc("b1", T.st0[:, :], T.nb[:, :], 32.0, OP.is_ge, -24.0, OP.mult)
+    sg("ctr", V.transpose(T.tt[:, 64:128], T.ts[:, 64:128]))
+    wt(V, "b1")
+    ttn("b2", T.hm[:, :], T.hi[:, :], T.m88[:, :], OP.mult)
+    tsc("b2", T.st[:, :], T.st0[:, :], 32.0, OP.add)
+    wt(V, "ctr")
+    sg("ctr", V.tensor_copy(T.tabt[:, :], T.tt[:, 64:128]))
+    wt(V, "b2")
+    ttn("b6", T.base[:, :], T.hm[:, :], T.nb[:, :], OP.add)
+    wt(S, "b6", "i7")
     for n in range(6):
         for q in range(2):
             j = 2 * n + q
-            tsc("b7", T.ln[:, 2 * M * n + q:2 * M * n + 2 * M:2], T.u24[:, 0:M], T.st[:, j:j + 1], OP.mult, T.base[:, j:j + 1], OP.add)
-
-    def spread(src, enc, dg, s_in, s_enc, s_dg, pb, s_pb, oh, s_oh):
-        wt(V, s_in)
-        tsc(s_enc, enc[:, :], src[:, :], T.g32[:, 0:1], OP.add)
-        wt(V, s_enc, "c5")
-        for q in range(2):
-            tsc(s_dg, dg[:, 128 * q:128 * q + 128], T.idb[:, :], enc[:, q:q + 1], OP.mult)
-        wt(TE, s_dg)
-        sg(s_pb, TE.matmul(pb[:, 0:256], T.ones[:, :], dg[:, :], True, True))
-        wt(V, s_pb)
-        for t in range(2):
-            tsc(s_oh, oh[:, 256 * t:256 * t + 256], pb[:, 0:256], T.kcol[:, t:t + 1], OP.is_equal)
-        wt(TE, s_oh)
-    wt(V, "m2")
-    for q in range(2):
-        sg("m3", V.tensor_reduce(T.a1[:, q:q + 1], T.mx[:, 32 * q:32 * q + 24], AxisListType.X, OP.add))
-    spread(T.a1, T.a1e, T.dg2, "m3", "m4", "d2", T.pb2, "p2", T.oh2, "o2")
+            sg("b3", S.activation(T.lnf[:, 2 * M * n + q:2 * M * n + 2 * M:2], T.u48[:, 0:M], AF.Identity, bias=T.base[:, j:j + 1],
+                                  scale=T.st[:, j:j + 1]))
+    compare(T.pb2, "p2", T.oh2, "o2")
+    wt(TE, "o2", "ctr")
     lookup("pC", T.psc, 64, T.oh2, T.tabt)
     lookup("pC", T.psc, 0, T.oh2, T.tabc)
-    wt(V, "pC")
     for q in range(2):
-        tsc("e1", T.mk2[:, 32 * q:32 * q + 24], T.psc[:, 64 + 32 * q:64 + 32 * q + 24], T.posf[:, q:q + 1], OP.is_equal)
+        tsc("c6", T.r16[:, q:q + 1], T.ri[:, 0:1], 16.0 * q, OP.add)
+    tsc("c6", T.lcs[:, 0:1], T.ri[:, 0:1], 32.0, OP.mult)
+    tsc("c6", T.lcs[:, 2:3], T.ri[:, 0:1], 32.0, OP.mult, 257.0, OP.add)
+    tsc("c6", T.w32[:, 1:2], T.wi[:, 0:1], -767.0, OP.mult, 512.0, OP.add)
+    wt(V, "pC", "afc")
     for q in range(2):
-        tsc("vly", T.ly[:, q:48:2], T.psc[:, 32 * q:32 * q + 24], 32.0, OP.mult, T.r16[:, q:q + 1], OP.add)
+        tsc("e1", T.mk2[:, 24 * q:24 * q + 24], T.psc[:, 64 + 24 * q:64 + 24 * q + 24], T.posf[:, q:q + 1], OP.is_equal)
+    wt(V, "c6")
+    ttn("c6", T.lcs[:, 1:2], T.lcs[:, 0:1], T.w32[:, 1:2], OP.add)
     wt(V, "e1")
+    ttn("e2", T.mx2[:, :], T.mk2[:, :], T.u48[:, :], OP.mult)
+    spread(T.mx2, T.my2, T.k1, T.dg3, "e2", "e3", "d3", T.pb3, "p3")
+    wt(V, "b3")
+    sg("b7", V.tensor_copy(T.ln[:, :], T.lnf[:, :]))
     for q in range(2):
-        ttn("e2", T.mx2[:, 32 * q:32 * q + 24], T.mk2[:, 32 * q:32 * q + 24], T.u24[:, :], OP.mult)
-    wt(V, "e2")
-    for q in range(2):
-        sg("e3", V.tensor_reduce(T.k1[:, q:q + 1], T.mx2[:, 32 * q:32 * q + 24], AxisListType.X, OP.add))
-    spread(T.k1, T.k1e, T.dg3, "e3", "e4", "d3", T.pb3, "p3", T.oh3, "o3")
+        tsc("vly", T.ly[:, q:48:2], T.psc[:, 24 * q:24 * q + 24], 32.0, OP.mult, T.r16[:, q:q + 1], OP.add)
+    wt(V, "c6")
+    for j in range(3):
+        tsc("j5", T.lc[:, j:48:3], T.m2i[:, :], T.lcs[:, j:j + 1], OP.add)
+    compare(T.pb3, "p3", T.oh3, "o3")
+    wt(TE, "o3")
     lookup("pD", T.psd, 0, T.oh3, T.tabc)
-    wt(V, "i5")
-    tsc("j1", T.jj[:, :], T.jt[:, :], T.g16[:, 0:1], OP.subtract)
-    wt(V, "j1")
-    tsc("j2", T.jm[:, :], T.jj[:, :], 2731.0, OP.mult)
-    tsc("j2", T.jb[:, :], T.jj[:, :], 32.0, OP.mult)
-    wt(V, "j2")
-    tsc("j3", T.ji[:, :], T.jm[:, :], 16, OP.arith_shift_right)
     wt(V, "pD")
     for q in range(2):
-        tsc("vl1", T.lf1[:, q:48:2], T.psd[:, 32 * q:32 * q + 24], 32.0, OP.mult, T.r16[:, q:q + 1], OP.add)
-    wt(V, "j3")
-    tsc("j4", T.ja[:, :], T.ji[:, :], -767.0, OP.mult)
-    wt(V, "j4")
-    ttn("j5", T.jc[:, :], T.ja[:, :], T.jb[:, :], OP.add)
-    wt(V, "j5")
-    sg("j5", V.tensor_copy(T.lc[:, :], T.jc[:, :]))
+        tsc("vl1", T.lf1[:, q:48:2], T.psd[:, 24 * q:24 * q + 24], 32.0, OP.mult, T.r16[:, q:q + 1], OP.add)
 
     wt(V, "b7", "vown")
     wt(S, "b7", "vown")
     for k in range(CH):
         maxima(0, k, T.n0)
-    gathers(1, 0, T.n0, T.lf1, ("aa00", "ab00", "aa01", "ab01", "vl1"))
-    gathers(1, 1, T.n0, T.lf1, ())
-    send(1, 0)
-    send(1, 1)
+    need = ["a%s0%d" % (h, k) for k in range(CH) for h in "ab"] + ["vl1"]
+    wt(V, *need)
+    wt(S, *need)
+    for k in range(CH):
+        own_chunk(1, k, T.n0, T.lf1)
+        slots(1, k)
+    for k in range(CH):
+        send(1, k)
     for k in range(CH):
         maxima(1, k, T.n1)
 
-    need = ("aa10", "ab10", "aa11", "ab11", "vly", "j5")
+    need = ["a%s1%d" % (h, k) for k in range(CH) for h in "ab"] + ["vly", "j5"]
     wt(V, *need)
     wt(S, *need)
     sg("y1", V.tensor_copy(T.yp[:, 0:384], T.n1[:, :].indirect(T.ly[:, 0:24])))

@@ -1,54 +1,51 @@
 from concourse.bass import DstId, RemoteDMATransfer
 from concourse.mybir import AluOpType as OP, ActivationFunctionType as AF
 
-NR, M = 8, 12
-CH = 24 // M
+NR, M, CH = 8, 12, 2
 OWN, REG = 32 * M, 8 * M
 WIN = OWN + NR * REG
 RK = [(r, k) for r in range(2) for k in range(CH)]
-RELAY = {rk: True for rk in RK}
+ZW = 240
+BANK = {(0, 4, 0): "pb1", (0, 4, 1): "pb2", (0, 5, 0): "pb3", (0, 5, 1): "psa",
+        (1, 4, 0): "psb", (1, 4, 1): "psc", (1, 5, 0): "psd", (1, 5, 1): "pb1"}
 
 F32, I32, U16, B16 = "float32", "int32", "uint16", "bfloat16"
+
+
+def _sb(n, t):
+    return ("sbuf", [128, n], t)
+
+
 SCRATCH = {
-    "xs": ("sbuf", [128, 768], F32), "n0": ("sbuf", [128, 768], F32), "n1": ("sbuf", [128, 768], F32),
-    "yp": ("sbuf", [128, 768], F32), "ys": ("sbuf", [128, 768], F32),
-    "ts": ("sbuf", [128, 128], I32), "tt": ("sbuf", [128, 128], I32), "tabr": ("sbuf", [128, 64], B16),
-    "tabc": ("sbuf", [128, 64], B16), "tabt": ("sbuf", [128, 64], B16),
-    "prow": ("sbuf", [128, 256], I32), "rowe": ("sbuf", [128, 256], B16),
-    "shi": ("sbuf", [128, 4], I32), "shf": ("sbuf", [128, 4], F32), "shx": ("sbuf", [128, 2 * M], B16),
-    "nb": ("sbuf", [128, 12], I32), "acti": ("sbuf", [128, 2], I32), "posi": ("sbuf", [128, 2], I32),
-    "actf": ("sbuf", [128, 2], F32), "posf": ("sbuf", [128, 2], F32),
-    "ones": ("sbuf", [128, 128], B16), "idb": ("sbuf", [128, 128], B16),
-    "rt": ("sbuf", [128, 128], F32), "rp": ("sbuf", [128, 256], B16),
-    "pidx": ("sbuf", [128, 2], I32), "ri": ("sbuf", [128, 2], I32), "wi": ("sbuf", [128, 2], I32),
-    "i24": ("sbuf", [128, 2], F32), "r16": ("sbuf", [128, 2], F32), "w32": ("sbuf", [128, 2], F32), "lcs": ("sbuf", [128, 4], F32),
-    "kcol": ("sbuf", [128, 2], F32), "rcb": ("sbuf", [128, 256], B16), "cwi": ("sbuf", [128, 4 * M], F32), "cwb": ("sbuf", [128, 4 * M], B16),
-    "u48": ("sbuf", [128, 48], F32), "m2i": ("sbuf", [128, 16], F32),
-    "lc": ("sbuf", [128, 48], U16), "lf0": ("sbuf", [128, 48], U16), "lf1": ("sbuf", [128, 48], U16), "ly": ("sbuf", [128, 48], U16),
-    "l0": ("sbuf", [128, 4 * M], U16), "ln": ("sbuf", [128, 12 * M], U16), "lnf": ("sbuf", [128, 12 * M], F32),
-    "oh": ("sbuf", [128, 512], B16), "oh2": ("sbuf", [128, 512], B16), "oh3": ("sbuf", [128, 512], B16),
-    "dg2": ("sbuf", [128, 256], B16), "dg3": ("sbuf", [128, 256], B16),
-    "hi": ("sbuf", [128, 12], I32), "m88": ("sbuf", [128, 12], F32), "st0": ("sbuf", [128, 12], F32), "st": ("sbuf", [128, 12], F32),
-    "hm": ("sbuf", [128, 12], F32), "base": ("sbuf", [128, 12], F32),
-    "mk": ("sbuf", [128, 48], F32), "mx": ("sbuf", [128, 48], F32), "my": ("sbuf", [128, 48], F32), "a1": ("sbuf", [128, 2], F32),
-    "mk2": ("sbuf", [128, 48], F32), "mx2": ("sbuf", [128, 48], F32), "my2": ("sbuf", [128, 48], F32), "k1": ("sbuf", [128, 2], F32),
+    "xs": _sb(768, F32), "n0": _sb(768, F32), "n1": _sb(768, F32), "ys": _sb(768, F32),
+    "ts": _sb(128, I32), "tt": _sb(128, I32), "tabr": _sb(64, B16), "tabc": _sb(64, B16), "tabt": _sb(64, B16),
+    "prow": _sb(256, I32), "rowe": _sb(256, B16), "shi": _sb(4, I32), "shf": _sb(4, F32), "shx": _sb(2 * M, B16),
+    "nb": _sb(12, I32), "acti": _sb(2, I32), "posi": _sb(2, I32), "actf": _sb(2, F32), "posf": _sb(2, F32),
+    "ones": _sb(128, B16), "idb": _sb(128, B16), "rt": _sb(128, F32), "rp": _sb(256, B16),
+    "pidx": _sb(2, I32), "ri": _sb(2, I32), "wi": _sb(2, I32), "i24": _sb(2, F32), "r16": _sb(2, F32), "w32": _sb(2, F32), "ww": _sb(2, F32),
+    "kcol": _sb(2, F32), "rcb": _sb(256, B16), "irow": _sb(32, B16), "cwi": _sb(4 * M, F32), "cwb": _sb(4 * M, B16), "u48": _sb(48, F32),
+    "lf0": _sb(48, U16), "lf1": _sb(48, U16), "ly": _sb(48, U16), "l0": _sb(4 * M, U16), "ln": _sb(12 * M, U16), "lnf": _sb(12 * M, F32),
+    "oh": _sb(512, B16), "oh2": _sb(512, B16), "oh3": _sb(512, B16), "dg2": _sb(256, B16), "dg3": _sb(256, B16), "zz": _sb(6 * ZW, B16),
+    "hi": _sb(12, I32), "m88": _sb(12, F32), "st0": _sb(12, F32), "st": _sb(12, F32), "hm": _sb(12, F32), "base": _sb(12, F32),
+    "mk": _sb(48, F32), "mx": _sb(48, F32), "my": _sb(48, F32), "a1": _sb(2, F32),
+    "mk2": _sb(48, F32), "mx2": _sb(48, F32), "my2": _sb(48, F32), "k1": _sb(2, F32), "ye": _sb(16, F32), "yo": _sb(16, F32), "yt": _sb(16, F32),
 }
 for _n in ("pb1", "psa", "psb", "pss", "pb2", "psc", "pb3", "psd"):
     SCRATCH[_n] = ("psum", [128, 512], F32)
-for _r, _k in RK:
-    SCRATCH["w%d%d" % (_r, _k)] = ("sbuf", [128, WIN], F32)
-    SCRATCH["s%d%d" % (_r, _k)] = ("sbuf", [128, 8 * REG], F32)
-    SCRATCH["q%d%d" % (_r, _k)] = ("sbuf", [128, OWN], F32)
-    SCRATCH["rl%d%d" % (_r, _k)] = ("sbuf", [128, 2 * REG], F32)
-SEMAPHORES = ["ms", "one", "vown", "i1", "i2", "i3", "i4", "i5", "i6", "i7", "c1", "c2", "c3", "c4", "c6", "j5",
+SEMAPHORES = ["ms", "one", "vown", "i1", "i2", "i3", "i4", "i5", "i6", "i7", "c1", "c2", "c3", "c4", "c6",
               "dp", "ds", "dr", "dx", "dc", "da", "dn", "dy", "row", "pb", "shc", "shx", "pS", "tr", "tab", "ohc", "pA", "pB", "vl0", "vlf",
               "ctr", "ctb", "afc", "m1", "m2", "m3", "d2", "p2", "o2", "pC", "vly", "e1", "e2", "e3", "d3", "p3", "o3", "pD", "vl1",
-              "b1", "b2", "b3", "b6", "b7", "y1", "y2a", "y2b", "lsem"]
+              "b1", "b2", "b3", "b6", "b7", "zf", "zc", "pY", "y1", "y3", "y2a", "y2b", "lsem"]
 for _r, _k in RK:
-    SEMAPHORES += [_s + "%d%d" % (_r, _k) for _s in ("f", "s", "arr", "rel", "na", "nb", "aa", "ab")]
+    SCRATCH["w%d%d" % (_r, _k)] = _sb(WIN, F32)
+    SCRATCH["s%d%d" % (_r, _k)] = _sb(8 * REG, F32)
+    SCRATCH["rl%d%d" % (_r, _k)] = _sb(2 * REG, F32)
+    for _j in (0, 4, 5):
+        SCRATCH["q%d%d%d" % (_j, _r, _k)] = _sb(OWN, F32)
+    SEMAPHORES += [_s + "%d%d" % (_r, _k) for _s in ("f", "s", "arr", "rel", "na", "nb", "aa", "ab", "ga", "gb", "ha", "hb", "ia", "ib")]
 
 
-def routes(src, rk, T, topo):
+def routes(src, T, topo):
     cores = T.cores
     c = cores[src]
     here = [p for p in range(NR) if p != src and topo.chip(cores[p]) == topo.chip(c)]
@@ -56,51 +53,34 @@ def routes(src, rk, T, topo):
 
     def place(p):
         return sum(1 for q in range(p) if topo.chip(cores[q]) == topo.chip(cores[p]))
-    relay = [p for p in away if not topo.same_plane(topo.chip(c), topo.chip(cores[p])) and place(p) == place(src)] if RELAY[rk] else []
+    relay = [p for p in away if not topo.same_plane(topo.chip(c), topo.chip(cores[p])) and place(p) == place(src)]
     direct = [p for p in away if p not in relay]
-    helper = None
-    if relay:
-        ok = [h for h in topo.cores_of(c) if topo.die(h) != topo.die(c) and all(topo.may_write(h, cores[p]) for p in relay)]
-        helper = ok[place(src)]
-    return direct, relay, here, helper
+    ok = [h for h in topo.cores_of(c) if topo.die(h) != topo.die(c) and all(topo.may_write(h, cores[p]) for p in relay)]
+    return direct, relay, here, ok[place(src)]
 
 
-def calls(src, rk, T, topo):
+def calls(src, T, topo):
     cores = T.cores
-    direct, relay, here, helper = routes(src, rk, T, topo)
+    direct, relay, here, helper = routes(src, T, topo)
     c = cores[src]
     off = topo.engines(c, cores[direct[0]])
     rest = [e for e in topo.engines(c, cores[here[0]]) if e not in off]
-    res = []
-    while direct:
-        part, direct = direct[:4], direct[4:]
-        n = len(off) // len(part)
-        call = [(p, cores[p], off[n * i:n * i + n]) for i, p in enumerate(part)]
-        if relay:
-            m = len(rest) // len(relay)
-            call += [(p, helper, rest[m * i:m * i + m]) for i, p in enumerate(relay)]
-            relay = []
-        res.append(call)
-    res.append([(p, cores[p], rest) for p in here])
-    return res
+    n, m = len(off) // len(direct), len(rest) // len(relay)
+    return [[(p, cores[p], off[n * i:n * i + n]) for i, p in enumerate(direct)]
+            + [(p, helper, rest[m * i:m * i + m]) for i, p in enumerate(relay)],
+            [(p, cores[p], rest) for p in here]]
 
 
-def hand_on(src, rk, T, topo):
-    _, relay, _, helper = routes(src, rk, T, topo)
-    if not relay:
-        return []
+def hand_on(src, T, topo):
+    _, relay, _, helper = routes(src, T, topo)
     off = topo.engines(helper, T.cores[relay[0]])
     n = len(off) // len(relay)
     return [(p, off[n * i:n * i + n]) for i, p in enumerate(relay)]
 
 
-def bits(engines):
-    return sum(1 << e for e in engines)
-
-
 def transfer(topo, dst, out, src, sem, engines):
     rid, pid, _ = topo.addr(dst)
-    return RemoteDMATransfer(dst_ids=[DstId(rid=rid, pnc=pid)], dma_engine_mask=bits(engines), remote_sem=sem, src=src, dst=out)
+    return RemoteDMATransfer(dst_ids=[DstId(rid=rid, pnc=pid)], dma_engine_mask=sum(1 << e for e in engines), remote_sem=sem, src=src, dst=out)
 
 
 def helper_program(g, core, T, topo):
@@ -108,10 +88,10 @@ def helper_program(g, core, T, topo):
     for r, k in RK:
         tag = "%d%d" % (r, k)
         for src in range(NR):
-            if routes(src, (r, k), T, topo)[3] != core:
+            if routes(src, T, topo)[3] != core:
                 continue
-            inc = sum(len(e) for call in calls(src, (r, k), T, topo) for p, c, e in call if c == core)
-            out = hand_on(src, (r, k), T, topo)
+            inc = sum(len(e) for call in calls(src, T, topo) for p, c, e in call if c == core)
+            out = hand_on(src, T, topo)
             g.wait_ge(T.sem["rel" + tag], inc)
             at = OWN + REG * src
             g.remote_dma_fused([transfer(topo, T.cores[p], T["w" + tag][:, at:at + REG], T["rl" + tag][:, REG * i:REG * i + REG],
@@ -147,6 +127,12 @@ def rank_program(g, core, T, topo):
     def ttn(sem, out, a, b, op):
         sg(sem, V.tensor_tensor(out, a, b, op))
 
+    def cpv(sem, out, a):
+        sg(sem, V.tensor_copy(out, a))
+
+    def cps(sem, out, a):
+        sg(sem, S.activation(out, a, AF.Copy))
+
     sg("ms", V.memset(T.ts[:, :], 0))
     sg("one", V.memset(T.ones[:, :], 1.0))
     sg("dp", Y.dma_start(T.prow[0:1, 0:256], T.pose[:, :]), 16)
@@ -178,7 +164,7 @@ def rank_program(g, core, T, topo):
     wt(g, "one")
     sg("i6", g.affine_select(T.idb[:, :], T.ones[:, :], [[-1, 128]], OP.is_equal, 0.0, 0, 1))
     iota("i7", T.u48[:, :], [[0, 2], [1, 24]], 0)
-    iota("i7", T.m2i[:, :], [[2, 16]], 0)
+    iota("i7", T.irow[0:1, :], [[1, 32]], 0)
     for r, k in RK:
         at = OWN + REG * rank
         iota("vown", T["w%d%d" % (r, k)][:, at:at + REG], [[0, REG]], 0)
@@ -198,17 +184,18 @@ def rank_program(g, core, T, topo):
     tsc("c4", T.cwb[:, :], T.cwi[:, :], T.w32[:, 0:1], OP.add)
 
     wt(V, "ds")
-    sg("shc", V.tensor_copy(T.shf[:, :], T.shi[:, :]))
+    cpv("shc", T.shf[:, :], T.shi[:, :])
     wt(S, "shc", "one")
     hm = M // 2
     for j in range(4):
         sg("shx", S.activation(T.shx[:, j * hm:j * hm + hm], T.ones[:, 0:hm], AF.Copy, scale=T.shf[:, j:j + 1]))
     wt(V, "dp")
     for q in range(2):
-        sg("row", V.tensor_copy(T.rowe[0:1, 128 * q:128 * q + 128], T.prow[0:1, q:256:2]))
+        cpv("row", T.rowe[0:1, 128 * q:128 * q + 128], T.prow[0:1, q:256:2])
 
-    def all_rows(sem, pb, lhs, rhs):
+    def all_rows(sem, pb, lhs, rhs, need):
         sg(sem, TE.matmul(pb[:, 0:256], T.ones[0:1, :], T.rcb[0:1, :], True, False))
+        wt(TE, need)
         sg(sem, TE.matmul(pb[:, 0:256], lhs, rhs, False, True))
 
     def compare(pb, s_pb, oh, s_oh):
@@ -221,8 +208,8 @@ def rank_program(g, core, T, topo):
             for t in range(2):
                 sg(sem, TE.matmul(ps[:, at + 24 * q:at + 24 * q + 24], oh[:, 256 * t + 128 * q:256 * t + 128 * q + 128],
                                   tab[:, 32 * t:32 * t + 24], t == 0, t == 1))
-    wt(TE, "one", "i3", "row")
-    all_rows("pb", T.pb1, T.ones[0:1, :], T.rowe[0:1, :])
+    wt(TE, "one", "i3")
+    all_rows("pb", T.pb1, T.ones[0:1, :], T.rowe[0:1, :], "row")
     wt(TE, "shx", "c3", "i6", "c4")
     for v in range(2):
         o = T.pss[:, 2 * M * v:2 * M * v + 2 * M]
@@ -230,44 +217,44 @@ def rank_program(g, core, T, topo):
         sg("pS", TE.matmul(o, T.idb[:, :], T.cwb[:, 2 * M * v:2 * M * v + 2 * M], False, True))
     wt(V, "dr")
     sg("tr", V.transpose(T.tt[:, 0:64], T.ts[:, 0:64]))
-    wt(V, "i5")
-    wt(V, "tr")
-    sg("tab", V.tensor_copy(T.tabr[:, :], T.tt[:, 0:64]))
+    wt(V, "i5", "tr")
+    cpv("tab", T.tabr[:, :], T.tt[:, 0:64])
     compare(T.pb1, "pb", T.oh, "ohc")
     wt(TE, "tab", "ohc")
     lookup("pA", T.psa, 0, T.oh, T.tabr)
     wt(V, "pS")
-    sg("vl0", V.tensor_copy(T.l0[:, :], T.pss[:, 0:4 * M]))
-    wt(V, "dc")
-    sg("ctb", V.tensor_copy(T.tabc[:, :], T.ts[:, 64:128]))
-    wt(TE, "ctb")
-    lookup("pB", T.psb, 0, T.oh, T.tabc)
+    cpv("vl0", T.l0[:, :], T.pss[:, 0:4 * M])
     wt(V, "pA")
     for q in range(2):
         tsc("vlf", T.lf0[:, q:48:2], T.psa[:, 24 * q:24 * q + 24], T.i24[:, q:q + 1], OP.add)
 
     H = OWN // 2
-    plan = {rk: calls(rank, rk, T, topo) for rk in RK}
+    plan = calls(rank, T, topo)
+    relayed = routes(rank, T, topo)[1]
+    arrivals = 0
+    for src in range(NR):
+        if src != rank:
+            arrivals += sum(len(e) for call in calls(src, T, topo) for p, c, e in call if p == rank and c == core)
+            arrivals += sum(len(e) for p, e in hand_on(src, T, topo) if p == rank)
 
     def own_chunk(r, k, win, lf):
         tag, c0 = "%d%d" % (r, k), 2 * M * k
         w = T["w" + tag]
-        sg("f" + tag, V.tensor_copy(w[:, 0:H], win[:, :].indirect(lf[:, c0:c0 + M])))
-        sg("f" + tag, S.activation(w[:, H:OWN], win[:, :].indirect(lf[:, c0 + M:c0 + 2 * M]), AF.Copy))
+        cpv("f" + tag, w[:, 0:H], win[:, :].indirect(lf[:, c0:c0 + M]))
+        cps("f" + tag, w[:, H:OWN], win[:, :].indirect(lf[:, c0 + M:c0 + 2 * M]))
 
     def slots(r, k):
         tag = "%d%d" % (r, k)
         w, s = T["w" + tag], T["s" + tag]
         wt(V, "f" + tag)
         wt(S, "f" + tag)
-        sg("s" + tag, V.tensor_copy(s[:, 0:4 * REG], w[:, 0:OWN].indirect(T.l0[:, 0:4 * hm])))
-        sg("s" + tag, S.activation(s[:, 4 * REG:8 * REG], w[:, 0:OWN].indirect(T.l0[:, 4 * hm:8 * hm]), AF.Copy))
+        cpv("s" + tag, s[:, 0:4 * REG], w[:, 0:OWN].indirect(T.l0[:, 0:4 * hm]))
+        cps("s" + tag, s[:, 4 * REG:8 * REG], w[:, 0:OWN].indirect(T.l0[:, 4 * hm:8 * hm]))
 
     def send(r, k):
         tag, at = "%d%d" % (r, k), OWN + REG * rank
-        relayed = routes(rank, (r, k), T, topo)[1]
         wt(g, "s" + tag)
-        for call in plan[(r, k)]:
+        for call in plan:
             tr = []
             for p, c, e in call:
                 i = 4 * (p % 2) + p // 2
@@ -280,42 +267,52 @@ def rank_program(g, core, T, topo):
                 cnt["lsem"] = cnt.get("lsem", 0) + len(e)
             g.remote_dma_fused(tr, local_sem=T.sem["lsem"])
 
-    def arrivals(r, k):
-        n = 0
-        for src in range(NR):
-            if src != rank:
-                n += sum(len(e) for call in calls(src, (r, k), T, topo) for p, c, e in call if p == rank and c == core)
-                n += sum(len(e) for p, e in hand_on(src, (r, k), T, topo) if p == rank)
-        return n
-
-    def maxima(r, k, out):
+    def maxima(r, k, out, middle=None):
         tag = "%d%d" % (r, k)
-        w, sq = T["w" + tag], T["q" + tag]
-        n = arrivals(r, k)
-        V.wait_ge(T.sem["arr" + tag], n)
-        S.wait_ge(T.sem["arr" + tag], n)
-        for h, s in enumerate(("na", "nb")):
-            sg(s + tag, S.activation(sq[:, H * h:H * h + H], w[:, :].indirect(T.ln[:, M * h:M * h + M]), AF.Copy))
-        for n in range(1, 6):
-            for h, (s, a) in enumerate((("na", "aa"), ("nb", "ab"))):
-                dst = out[:, OWN * k + H * h:OWN * k + H * h + H]
-                wt(V, (s if n == 1 else a) + tag)
-                ttn(a + tag, dst, w[:, :].indirect(T.ln[:, 2 * M * n + M * h:2 * M * n + M * h + M]),
-                    sq[:, H * h:H * h + H] if n == 1 else dst, OP.max)
+        w = T["w" + tag]
+        for q in (V, S):
+            q.wait_ge(T.sem["arr" + tag], arrivals)
+
+        def pick(j, h):
+            return w[:, :].indirect(T.ln[:, 2 * M * j + M * h:2 * M * j + M * h + M])
+        halves = [(h, "ab"[h], slice(H * h, H * h + H), out[:, OWN * k + H * h:OWN * k + H * h + H]) for h in range(2)]
+        for j, s in ((0, "n"), (4, "g"), (5, "g")):
+            for h, a, c, dst in halves:
+                cps(s + a + tag, T["q%d%s" % (j, tag)][:, c], pick(j, h))
+            for h, a, c, dst in halves:
+                if j:
+                    wt(S, "g" + a + tag)
+                    if (k, j, h) == (1, 5, 0):
+                        wt(S, "vl1")
+                    if (k, j, h) == (1, 5, 1):
+                        wt(S, "aa%d0" % r)
+                    cps(("h" if j == 4 else "i") + a + tag, T[BANK[(k, j, h)]][:, 0:H], T["q%d%s" % (j, tag)][:, c])
+        for j in range(1, 6):
+            if j == 3 and middle:
+                middle()
+            for h, a, c, dst in halves:
+                wt(V, ("n" if j == 1 else "a") + a + tag)
+                if j < 4:
+                    ttn("a" + a + tag, dst, pick(j, h), T["q0" + tag][:, c] if j == 1 else dst, OP.max)
+                else:
+                    wt(V, ("h" if j == 4 else "i") + a + tag)
+                    ttn("a" + a + tag, dst, T[BANK[(k, j, h)]][:, 0:H], dst, OP.max)
 
     wt(V, "vlf", "dx", "vl0")
     wt(S, "vlf", "dx", "vl0")
     own_chunk(0, 0, T.xs, T.lf0)
     slots(0, 0)
-    for k in range(1, CH):
-        own_chunk(0, k, T.xs, T.lf0)
+    own_chunk(0, 1, T.xs, T.lf0)
+    wt(V, "dc")
+    cpv("ctb", T.tabc[:, :], T.ts[:, 64:128])
+    wt(TE, "ctb")
+    lookup("pB", T.psb, 0, T.oh, T.tabc)
     wt(V, "da")
-    sg("afc", V.tensor_copy(T.actf[:, :], T.acti[:, :]))
-    sg("afc", V.tensor_copy(T.posf[:, :], T.posi[:, :]))
-    for k in range(1, CH):
-        slots(0, k)
-    for k in range(CH):
-        send(0, k)
+    cpv("afc", T.actf[:, :], T.acti[:, :])
+    cpv("afc", T.posf[:, :], T.posi[:, :])
+    slots(0, 1)
+    send(0, 0)
+    send(0, 1)
 
     wt(V, "afc", "i7")
     for q in range(2):
@@ -331,8 +328,7 @@ def rank_program(g, core, T, topo):
         wt(S, s_num, "i6")
         for q in range(2):
             sg(s_dg, S.activation(dg[:, 128 * q:128 * q + 128], T.idb[:, :], AF.Copy, scale=num[:, q:q + 1]))
-        wt(TE, s_dg)
-        all_rows(s_pb, pb, T.ones[:, :], dg[:, :])
+        all_rows(s_pb, pb, T.ones[:, :], dg[:, :], s_dg)
     spread(T.mx, T.my, T.a1, T.dg2, "m2", "m3", "d2", T.pb2, "p2")
     wt(V, "dn")
     tsc("b1", T.hi[:, :], T.nb[:, :], 3, OP.arith_shift_right)
@@ -343,7 +339,7 @@ def rank_program(g, core, T, topo):
     ttn("b2", T.hm[:, :], T.hi[:, :], T.m88[:, :], OP.mult)
     tsc("b2", T.st[:, :], T.st0[:, :], 32.0, OP.add)
     wt(V, "ctr")
-    sg("ctr", V.tensor_copy(T.tabt[:, :], T.tt[:, 64:128]))
+    cpv("ctr", T.tabt[:, :], T.tt[:, 64:128])
     wt(V, "b2")
     ttn("b6", T.base[:, :], T.hm[:, :], T.nb[:, :], OP.add)
     wt(S, "b6", "i7")
@@ -354,59 +350,71 @@ def rank_program(g, core, T, topo):
                                   scale=T.st[:, j:j + 1]))
     compare(T.pb2, "p2", T.oh2, "o2")
     wt(TE, "o2", "ctr")
-    lookup("pC", T.psc, 64, T.oh2, T.tabt)
-    lookup("pC", T.psc, 0, T.oh2, T.tabc)
+    lookup("pC", T.psc, 0, T.oh2, T.tabt)
     for q in range(2):
         tsc("c6", T.r16[:, q:q + 1], T.ri[:, 0:1], 16.0 * q, OP.add)
-    tsc("c6", T.lcs[:, 0:1], T.ri[:, 0:1], 32.0, OP.mult)
-    tsc("c6", T.lcs[:, 2:3], T.ri[:, 0:1], 32.0, OP.mult, 257.0, OP.add)
-    tsc("c6", T.w32[:, 1:2], T.wi[:, 0:1], -767.0, OP.mult, 512.0, OP.add)
+        tsc("c6", T.ww[:, q:q + 1], T.wi[:, 0:1], 2.0 * q - 1.0, OP.mult, 1.0 - q, OP.add)
     wt(V, "pC", "afc")
     for q in range(2):
-        tsc("e1", T.mk2[:, 24 * q:24 * q + 24], T.psc[:, 64 + 24 * q:64 + 24 * q + 24], T.posf[:, q:q + 1], OP.is_equal)
-    wt(V, "c6")
-    ttn("c6", T.lcs[:, 1:2], T.lcs[:, 0:1], T.w32[:, 1:2], OP.add)
+        tsc("e1", T.mk2[:, 24 * q:24 * q + 24], T.psc[:, 24 * q:24 * q + 24], T.posf[:, q:q + 1], OP.is_equal)
     wt(V, "e1")
     ttn("e2", T.mx2[:, :], T.mk2[:, :], T.u48[:, :], OP.mult)
     spread(T.mx2, T.my2, T.k1, T.dg3, "e2", "e3", "d3", T.pb3, "p3")
+    sg("zf", V.memset(T.zz[:, :], 0.0))
+    wt(S, "zf", "ctb")
+    for t in range(2):
+        for n, (a, b, o) in ((0, (0, 16, 0)), (1, (16, 24, 0)), (1, (0, 8, 8)), (2, (8, 24, 0))):
+            z = ZW * (3 * t + n) + 112 + o
+            sg("zc", S.activation(T.zz[:, z:z + b - a], T.tabc[:, 32 * t + a:32 * t + b], AF.Copy, scale=32.0))
     wt(V, "b3")
-    sg("b7", V.tensor_copy(T.ln[:, :], T.lnf[:, :]))
-    for q in range(2):
-        tsc("vly", T.ly[:, q:48:2], T.psc[:, 24 * q:24 * q + 24], 32.0, OP.mult, T.r16[:, q:q + 1], OP.add)
-    wt(V, "c6")
-    for j in range(3):
-        tsc("j5", T.lc[:, j:48:3], T.m2i[:, :], T.lcs[:, j:j + 1], OP.add)
+    cpv("b7", T.ln[:, :], T.lnf[:, :])
     compare(T.pb3, "p3", T.oh3, "o3")
     wt(TE, "o3")
     lookup("pD", T.psd, 0, T.oh3, T.tabc)
-    wt(V, "pD")
-    for q in range(2):
-        tsc("vl1", T.lf1[:, q:48:2], T.psd[:, 24 * q:24 * q + 24], 32.0, OP.mult, T.r16[:, q:q + 1], OP.add)
+
+    def next_list():
+        wt(V, "pD", "c6")
+        for q in range(2):
+            tsc("vl1", T.lf1[:, q:48:2], T.psd[:, 24 * q:24 * q + 24], 32.0, OP.mult, T.r16[:, q:q + 1], OP.add)
+    wt(TE, "zc", "vl0", "i7")
+    for n in range(3):
+        for q in range(2):
+            o = T.pss[:, 32 * n + 16 * q:32 * n + 16 * q + 16]
+            sg("pY", TE.matmul(o, T.ones[0:1, :], T.irow[0:1, 16 * q:16 * q + 16], True, False))
+            for gr in range(8):
+                t = gr // 4
+                z = ZW * (3 * t + n) + 112 - 16 * gr
+                c = 256 * t + 128 * q + 16 * gr
+                sg("pY", TE.matmul(o, T.zz[:, z:z + 128], T.oh2[:, c:c + 16], False, gr == 7))
 
     wt(V, "b7", "vown")
-    wt(S, "b7", "vown")
-    for k in range(CH):
-        maxima(0, k, T.n0)
-    need = ["a%s0%d" % (h, k) for k in range(CH) for h in "ab"] + ["vl1"]
-    wt(V, *need)
-    wt(S, *need)
+    wt(S, "b7", "vown", "o3")
+    maxima_sems = [["a%s%d%d" % (h, r, k) for k in range(CH) for h in "ab"] for r in range(2)]
+    maxima(0, 0, T.n0, next_list)
+    maxima(0, 1, T.n0)
+    wt(V, "vl1", *maxima_sems[0])
+    wt(S, "vl1", *maxima_sems[0])
     for k in range(CH):
         own_chunk(1, k, T.n0, T.lf1)
         slots(1, k)
     for k in range(CH):
         send(1, k)
+    wt(V, "pY", "c6")
+    cpv("vly", T.ly[:, 0:48:3], T.pss[:, 0:32:2])
+    cpv("vly", T.ly[:, 2:48:3], T.pss[:, 65:96:2])
+    tsc("y1", T.ye[:, :], T.pss[:, 32:64:2], T.ww[:, 0:1], OP.mult)
+    tsc("y1", T.yo[:, :], T.pss[:, 33:64:2], T.ww[:, 1:2], OP.mult)
+    wt(V, "y1")
+    ttn("y3", T.yt[:, :], T.ye[:, :], T.yo[:, :], OP.add)
+    wt(V, "y3")
+    cpv("vly", T.ly[:, 1:48:3], T.yt[:, :])
     for k in range(CH):
         maxima(1, k, T.n1)
 
-    need = ["a%s1%d" % (h, k) for k in range(CH) for h in "ab"] + ["vly", "j5"]
-    wt(V, *need)
-    wt(S, *need)
-    sg("y1", V.tensor_copy(T.yp[:, 0:384], T.n1[:, :].indirect(T.ly[:, 0:24])))
-    sg("y1", S.activation(T.yp[:, 384:768], T.n1[:, :].indirect(T.ly[:, 24:48]), AF.Copy))
-    wt(V, "y1")
-    wt(S, "y1")
-    sg("y2a", V.tensor_copy(T.ys[:, 0:384], T.yp[:, :].indirect(T.lc[:, 0:24])))
-    sg("y2b", S.activation(T.ys[:, 384:768], T.yp[:, :].indirect(T.lc[:, 24:48]), AF.Copy))
+    wt(V, "vly", *maxima_sems[1])
+    wt(S, "vly", *maxima_sems[1])
+    cpv("y2a", T.ys[:, 0:384], T.n1[:, :].indirect(T.ly[:, 0:24]))
+    cps("y2b", T.ys[:, 384:768], T.n1[:, :].indirect(T.ly[:, 24:48]))
     wt(Y, "y2a")
     sg("dy", Y.dma_start(T.y[:, 0:384], T.ys[:, 0:384]), 16)
     wt(S, "y2b")

@@ -1,13 +1,17 @@
 from concourse.bass import DstId, RemoteDMATransfer
-from concourse.mybir import AluOpType as OP, ActivationFunctionType as AF
+from concourse.mybir import AluOpType as OP, ActivationFunctionType as AF, AxisListType as AX
 
 NR, M, CH = 8, 12, 2
 OWN, REG = 32 * M, 8 * M
 WIN = OWN + NR * REG
+HM = M // 2
 RK = [(r, k) for r in range(2) for k in range(CH)]
-ZW = 240
-BANK = {(0, 4, 0): "pb1", (0, 4, 1): "pb2", (0, 5, 0): "pb3", (0, 5, 1): "psa",
-        (1, 4, 0): "psb", (1, 4, 1): "psc", (1, 5, 0): "psd", (1, 5, 1): "pb1"}
+NEAR = (1,)
+PICKS = (("sr", HM, 2 * HM, 3 * HM), ("s", 3 * HM, 6 * HM - 2, NR * HM))
+ZT = 112 + 6 * 128
+BANKS = ("pb1", "pb2", "pb3", "psa", "psb", "psc", "psd")
+ORDER = ((4, "b", "b", 1), (4, "a", "a", 0), (3, "c", "b", 1), (5, "a", "a", 0), (5, "b", "b", 1))
+TAKE = (0, 1, 4, 3, 2)
 
 F32, I32, U16, B16 = "float32", "int32", "uint16", "bfloat16"
 
@@ -19,33 +23,36 @@ def _sb(n, t):
 SCRATCH = {
     "xs": _sb(768, F32), "n0": _sb(768, F32), "n1": _sb(768, F32), "ys": _sb(768, F32),
     "ts": _sb(128, I32), "tt": _sb(128, I32), "tabr": _sb(64, B16), "tabc": _sb(64, B16), "tabt": _sb(64, B16),
-    "prow": _sb(256, I32), "rowe": _sb(256, B16), "shi": _sb(4, I32), "shf": _sb(4, F32), "shx": _sb(2 * M, B16),
+    "prow": _sb(256, I32), "rowe": _sb(256, B16), "shi": _sb(4, I32), "shf": _sb(4, F32), "shx": _sb(4 * HM, B16),
     "nb": _sb(12, I32), "acti": _sb(2, I32), "posi": _sb(2, I32), "actf": _sb(2, F32), "posf": _sb(2, F32),
-    "ones": _sb(128, B16), "idb": _sb(128, B16), "rt": _sb(128, F32), "rp": _sb(256, B16),
+    "ones": _sb(128, B16), "idb": _sb(128, B16), "idf": _sb(128, F32), "rp": _sb(256, B16),
     "pidx": _sb(2, I32), "ri": _sb(2, I32), "wi": _sb(2, I32), "i24": _sb(2, F32), "r16": _sb(2, F32), "w32": _sb(2, F32), "ww": _sb(2, F32),
-    "kcol": _sb(2, F32), "rcb": _sb(256, B16), "irow": _sb(32, B16), "cwi": _sb(4 * M, F32), "cwb": _sb(4 * M, B16), "u48": _sb(48, F32),
-    "lf0": _sb(48, U16), "lf1": _sb(48, U16), "ly": _sb(48, U16), "l0": _sb(4 * M, U16), "ln": _sb(12 * M, U16), "lnf": _sb(12 * M, F32),
-    "oh": _sb(512, B16), "oh2": _sb(512, B16), "oh3": _sb(512, B16), "dg2": _sb(256, B16), "dg3": _sb(256, B16), "zz": _sb(6 * ZW, B16),
+    "kcol": _sb(2, F32), "rcb": _sb(256, B16), "irow": _sb(32, B16), "cwi": _sb(4 * HM, F32), "cwb": _sb(4 * HM, B16), "u48": _sb(48, F32),
+    "lf0": _sb(48, U16), "lf1": _sb(48, U16), "ly": _sb(48, U16), "l0": _sb(8 * HM, U16), "ln": _sb(12 * M, U16), "lnf": _sb(6 * M, F32),
+    "oh": _sb(256, B16), "oh2": _sb(256, B16), "ohy": _sb(256, B16), "oh3": _sb(256, B16), "dg2": _sb(256, B16), "dg3": _sb(256, B16),
+    "zz": _sb(ZT, B16),
     "hi": _sb(12, I32), "m88": _sb(12, F32), "st0": _sb(12, F32), "st": _sb(12, F32), "hm": _sb(12, F32), "base": _sb(12, F32),
-    "mk": _sb(48, F32), "mx": _sb(48, F32), "my": _sb(48, F32), "a1": _sb(2, F32),
-    "mk2": _sb(48, F32), "mx2": _sb(48, F32), "my2": _sb(48, F32), "k1": _sb(2, F32), "ye": _sb(16, F32), "yo": _sb(16, F32), "yt": _sb(16, F32),
+    "mk": _sb(48, F32), "mx": _sb(48, F32), "a1": _sb(2, F32),
+    "mk2": _sb(48, F32), "mx2": _sb(48, F32), "k1": _sb(2, F32), "ye": _sb(16, F32), "yo": _sb(16, F32), "yt": _sb(16, F32),
 }
-for _n in ("pb1", "psa", "psb", "pss", "pb2", "psc", "pb3", "psd"):
+for _n in ("pss",) + BANKS:
     SCRATCH[_n] = ("psum", [128, 512], F32)
-SEMAPHORES = ["ms", "one", "vown", "i1", "i2", "i3", "i4", "i5", "i6", "i7", "c1", "c2", "c3", "c4", "c6",
-              "dp", "ds", "dr", "dx", "dc", "da", "dn", "dy", "row", "pb", "shc", "shx", "pS", "tr", "tab", "ohc", "pA", "pB", "vl0", "vlf",
-              "ctr", "ctb", "afc", "m1", "m2", "m3", "d2", "p2", "o2", "pC", "vly", "e1", "e2", "e3", "d3", "p3", "o3", "pD", "vl1",
-              "b1", "b2", "b3", "b6", "b7", "zf", "zc", "pY", "y1", "y3", "y2a", "y2b", "lsem"]
+SEMAPHORES = ["ms", "mt", "one", "zf", "vown", "i1", "i3", "i4", "i5", "i6", "i7", "irp", "c1", "c2", "c4", "c6", "c7",
+              "dp", "ds", "dr", "dx", "dc", "da", "dn", "dy", "row0", "row1", "pb0", "pb1", "shc", "shx", "pS", "tr", "tab",
+              "oh0", "oh1", "pA0", "pA1", "pB", "vl0", "vlf",
+              "ctr", "ctb", "afc", "m1", "m2", "m3", "d2", "p2", "o2", "oy", "pC", "vly", "e1", "e2", "e3", "d3", "p3", "o3", "pD", "vl1",
+              "b1", "b2", "b3", "b6", "b7", "idf", "zc", "pY", "y1", "y3", "y2a", "y2b", "lsem"]
 for _r, _k in RK:
     SCRATCH["w%d%d" % (_r, _k)] = _sb(WIN, F32)
-    SCRATCH["s%d%d" % (_r, _k)] = _sb(8 * REG, F32)
+    SCRATCH["s%d%d" % (_r, _k)] = _sb(NR * REG, F32)
     SCRATCH["rl%d%d" % (_r, _k)] = _sb(2 * REG, F32)
-    for _j in (0, 4, 5):
+    for _j in (0, 3, 4, 5):
         SCRATCH["q%d%d%d" % (_j, _r, _k)] = _sb(OWN, F32)
-    SEMAPHORES += [_s + "%d%d" % (_r, _k) for _s in ("f", "s", "arr", "rel", "na", "nb", "aa", "ab", "ga", "gb", "ha", "hb", "ia", "ib")]
+    SEMAPHORES += [_s + "%d%d" % (_r, _k) for _s in ("f", "sr", "s", "arr", "rel", "na", "nb", "aa", "ab", "ga", "gb", "gc", "ha", "hb", "hc",
+                                                     "ua", "ub", "ia", "ib")]
 
 
-def routes(src, T, topo):
+def routes(src, k, T, topo):
     cores = T.cores
     c = cores[src]
     here = [p for p in range(NR) if p != src and topo.chip(cores[p]) == topo.chip(c)]
@@ -53,29 +60,40 @@ def routes(src, T, topo):
 
     def place(p):
         return sum(1 for q in range(p) if topo.chip(cores[q]) == topo.chip(cores[p]))
-    relay = [p for p in away if not topo.same_plane(topo.chip(c), topo.chip(cores[p])) and place(p) == place(src)]
-    direct = [p for p in away if p not in relay]
-    ok = [h for h in topo.cores_of(c) if topo.die(h) != topo.die(c) and all(topo.may_write(h, cores[p]) for p in relay)]
-    return direct, relay, here, ok[place(src)]
+    same = [p for p in away if place(p) == place(src)]
+    near = [p for p in same if topo.same_plane(topo.chip(c), topo.chip(cores[p]))]
+    far = [p for p in same if p not in near]
+    others = [h for h in topo.cores_of(c) if topo.die(h) != topo.die(c)]
+    owners = [h for h in others if all(topo.may_write(h, cores[p]) for p in far)]
+    plain = [h for h in others if h not in owners]
+    handed = {owners[place(src)]: far}
+    if k in NEAR:
+        handed[plain[place(src)]] = near
+    return [p for p in away if not any(p in v for v in handed.values())], handed, here
 
 
-def calls(src, T, topo):
+def calls(src, r, k, T, topo):
     cores = T.cores
-    direct, relay, here, helper = routes(src, T, topo)
+    direct, handed, here = routes(src, k, T, topo)
     c = cores[src]
     off = topo.engines(c, cores[direct[0]])
     rest = [e for e in topo.engines(c, cores[here[0]]) if e not in off]
-    n, m = len(off) // len(direct), len(rest) // len(relay)
-    return [[(p, cores[p], off[n * i:n * i + n]) for i, p in enumerate(direct)]
-            + [(p, helper, rest[m * i:m * i + m]) for i, p in enumerate(relay)],
-            [(p, cores[p], rest) for p in here]]
+    first, second = [], [(p, cores[p], off[2 * i:2 * i + 2]) for i, p in enumerate(direct)]
+    second += [(p, cores[p], off[2 * len(direct):] or rest) for p in here]
+    for n, (h, ranks) in enumerate(handed.items()):
+        use = topo.engines(c, h) if n == 0 and (r, k) == (1, 0) else rest
+        m = len(use) // len(ranks)
+        (second if n else first).extend((p, h, use[m * i:m * i + m]) for i, p in enumerate(ranks))
+    return [first, second]
 
 
-def hand_on(src, T, topo):
-    _, relay, _, helper = routes(src, T, topo)
-    off = topo.engines(helper, T.cores[relay[0]])
-    n = len(off) // len(relay)
-    return [(p, off[n * i:n * i + n]) for i, p in enumerate(relay)]
+def hand_on(src, k, T, topo):
+    res = {}
+    for h, ranks in routes(src, k, T, topo)[1].items():
+        off = topo.engines(h, T.cores[ranks[0]])
+        n = len(off) // len(ranks)
+        res[h] = [(p, off[n * i:n * i + n]) for i, p in enumerate(ranks)]
+    return res
 
 
 def transfer(topo, dst, out, src, sem, engines):
@@ -88,11 +106,10 @@ def helper_program(g, core, T, topo):
     for r, k in RK:
         tag = "%d%d" % (r, k)
         for src in range(NR):
-            if routes(src, T, topo)[3] != core:
+            out = hand_on(src, k, T, topo).get(core)
+            if not out:
                 continue
-            inc = sum(len(e) for call in calls(src, T, topo) for p, c, e in call if c == core)
-            out = hand_on(src, T, topo)
-            g.wait_ge(T.sem["rel" + tag], inc)
+            g.wait_ge(T.sem["rel" + tag], sum(len(e) for call in calls(src, r, k, T, topo) for p, c, e in call if c == core))
             at = OWN + REG * src
             g.remote_dma_fused([transfer(topo, T.cores[p], T["w" + tag][:, at:at + REG], T["rl" + tag][:, REG * i:REG * i + REG],
                                          T.sem["arr" + tag], e) for i, (p, e) in enumerate(out)], local_sem=T.sem["lsem"])
@@ -133,8 +150,9 @@ def rank_program(g, core, T, topo):
     def cps(sem, out, a):
         sg(sem, S.activation(out, a, AF.Copy))
 
-    sg("ms", V.memset(T.ts[:, :], 0))
+    sg("ms", V.memset(T.ts[:, 0:64], 0))
     sg("one", V.memset(T.ones[:, :], 1.0))
+    sg("mt", V.memset(T.ts[:, 64:128], 0))
     sg("dp", Y.dma_start(T.prow[0:1, 0:256], T.pose[:, :]), 16)
     sg("ds", S.dma_start(T.shi[:, :], T.shown[:, :]), 16)
     wt(Y, "ms")
@@ -144,12 +162,13 @@ def rank_program(g, core, T, topo):
             q = Y if gg < 2 else S
             sg("dr", q.dma_start(T.ts[32 * gg:32 * gg + 24, 32 * t:32 * t + 24], T.rel[4 * t + gg:4 * t + gg + 1, :]), 16)
     sg("dx", S.dma_start(T.xs[:, :], T.x[:, :]), 16)
-    sg("da", S.dma_start(T.posi[:, :], T.pose[:, :]), 16)
-    sg("da", Y.dma_start(T.acti[:, :], T.act[:, :]), 16)
+    wt(Y, "mt")
     for t in range(2):
         for gg in range(4):
             sg("dc", Y.dma_start(T.ts[32 * gg:32 * gg + 24, 64 + 32 * t:64 + 32 * t + 24], T.ct[4 * t + gg:4 * t + gg + 1, :]), 16)
-    sg("dn", Y.dma_start(T.nb[:, :], T.nbr[:, :]), 16)
+    sg("da", Y.dma_start(T.posi[:, :], T.pose[:, :]), 16)
+    sg("da", Y.dma_start(T.acti[:, :], T.act[:, :]), 16)
+    sg("dn", S.dma_start(T.nb[:, :], T.nbr[:, :]), 16)
 
     def iota(sem, out, pattern, cm, flag=True):
         if flag:
@@ -157,14 +176,15 @@ def rank_program(g, core, T, topo):
         else:
             sg(sem, g.iota(out, pattern, 0, cm))
     iota("i1", T.pidx[:, 0:1], [[0, 1]], 1, False)
-    iota("i2", T.rt[:, :], [[-16, 8], [0, 2], [-1, 8]], 1)
-    iota("i3", T.rcb[0:1, :], [[0, 2], [32, 8], [0, 16]], 0)
-    iota("i4", T.cwi[:, :], [[0, 8], [64, M // 2]], 0)
-    iota("i5", T.kcol[:, :], [[128, 2]], 1)
+    iota("i4", T.cwi[:, :], [[0, 4], [64, HM]], 0)
+    iota("i5", T.kcol[:, 0:1], [[0, 1]], 1)
+    iota("i3", T.rcb[0:1, :], [[0, 4], [32, 4], [0, 16]], 0)
     wt(g, "one")
+    for v in range(2):
+        sg("irp", g.affine_select(T.rp[:, 128 * v:128 * v + 128], T.ones[:, :], [[-16, 8], [0, 2], [-1, 8]], OP.is_equal, 0.0, -8 * v, 1))
     sg("i6", g.affine_select(T.idb[:, :], T.ones[:, :], [[-1, 128]], OP.is_equal, 0.0, 0, 1))
     iota("i7", T.u48[:, :], [[0, 2], [1, 24]], 0)
-    iota("i7", T.irow[0:1, :], [[1, 32]], 0)
+    iota("i7", T.irow[0:1, :], [[1, 16], [16, 2]], 0)
     for r, k in RK:
         at = OWN + REG * rank
         iota("vown", T["w%d%d" % (r, k)][:, at:at + REG], [[0, REG]], 0)
@@ -173,69 +193,72 @@ def rank_program(g, core, T, topo):
     p1 = T.pidx[:, 0:1]
     tsc("c1", T.ri[:, 0:1], p1, 15, OP.bitwise_and)
     tsc("c1", T.wi[:, 0:1], p1, 3, OP.arith_shift_right, 1, OP.bitwise_and)
-    wt(V, "i2")
-    for v in range(2):
-        tsc("c3", T.rp[:, 128 * v:128 * v + 128], T.rt[:, :], 8.0 * v, OP.is_equal)
+    sg("zf", V.memset(T.zz[:, :], 0.0))
     wt(V, "c1")
+    cpv("c2", T.r16[:, 0:1], T.ri[:, 0:1])
     tsc("c2", T.w32[:, 0:1], T.wi[:, 0:1], 32.0, OP.mult)
-    for q in range(2):
-        tsc("c2", T.i24[:, q:q + 1], T.ri[:, 0:1], 24.0, OP.mult, 384.0 * q, OP.add)
-    wt(V, "i4", "c2")
+    wt(V, "c2", "i4")
     tsc("c4", T.cwb[:, :], T.cwi[:, :], T.w32[:, 0:1], OP.add)
+    wt(S, "c2")
+    for q in range(2):
+        sg("c6", S.activation(T.i24[:, q:q + 1], T.r16[:, 0:1], AF.Copy, bias=384.0 * q, scale=24.0))
 
-    wt(V, "ds")
-    cpv("shc", T.shf[:, :], T.shi[:, :])
-    wt(S, "shc", "one")
-    hm = M // 2
-    for j in range(4):
-        sg("shx", S.activation(T.shx[:, j * hm:j * hm + hm], T.ones[:, 0:hm], AF.Copy, scale=T.shf[:, j:j + 1]))
     wt(V, "dp")
     for q in range(2):
-        cpv("row", T.rowe[0:1, 128 * q:128 * q + 128], T.prow[0:1, q:256:2])
+        cpv("row%d" % q, T.rowe[0:1, 128 * q:128 * q + 128], T.prow[0:1, q:256:2])
+    wt(V, "ds")
+    cpv("shc", T.shf[:, :], T.shi[:, :])
+    js = [rank // 2] + [p // 2 for v in routes(rank, 0, T, topo)[1].values() for p in v]
+    js += [j for j in range(NR // 2) if j not in js]
+    order = [2 * j + v for v in (rank % 2, 1 - rank % 2) for j in js]
+    wt(S, "shc", "one")
+    for i, j in enumerate(js):
+        sg("shx", S.activation(T.shx[:, i * HM:i * HM + HM], T.ones[:, 0:HM], AF.Copy, scale=T.shf[:, j:j + 1]))
 
-    def all_rows(sem, pb, lhs, rhs, need):
-        sg(sem, TE.matmul(pb[:, 0:256], T.ones[0:1, :], T.rcb[0:1, :], True, False))
-        wt(TE, need)
-        sg(sem, TE.matmul(pb[:, 0:256], lhs, rhs, False, True))
-
-    def compare(pb, s_pb, oh, s_oh):
-        wt(V, s_pb)
+    def lookup(sem, ps, oh, tab, q, at):
         for t in range(2):
-            tsc(s_oh, oh[:, 256 * t:256 * t + 256], pb[:, 0:256], T.kcol[:, t:t + 1], OP.is_equal)
-
-    def lookup(sem, ps, at, oh, tab):
-        for q in range(2):
-            for t in range(2):
-                sg(sem, TE.matmul(ps[:, at + 24 * q:at + 24 * q + 24], oh[:, 256 * t + 128 * q:256 * t + 128 * q + 128],
-                                  tab[:, 32 * t:32 * t + 24], t == 0, t == 1))
+            sg(sem, TE.matmul(ps[64 * t:64 * t + 64, at:at + 24], oh[:, 128 * q + 64 * t:128 * q + 64 * t + 64],
+                              tab[:, 32 * t:32 * t + 24], True, True))
+    first = ((T.pb1, T.psa), (T.pb2, T.psc))
     wt(TE, "one", "i3")
-    all_rows("pb", T.pb1, T.ones[0:1, :], T.rowe[0:1, :], "row")
-    wt(TE, "shx", "c3", "i6", "c4")
-    for v in range(2):
-        o = T.pss[:, 2 * M * v:2 * M * v + 2 * M]
-        sg("pS", TE.matmul(o, T.rp[:, 128 * v:128 * v + 128], T.shx[:, :], True, False))
-        sg("pS", TE.matmul(o, T.idb[:, :], T.cwb[:, 2 * M * v:2 * M * v + 2 * M], False, True))
+    for q in range(2):
+        c = slice(128 * q, 128 * q + 128)
+        sg("pb%d" % q, TE.matmul(first[q][0][:, 0:128], T.ones[0:1, :], T.rcb[0:1, c], True, False))
+    for q in range(2):
+        c = slice(128 * q, 128 * q + 128)
+        wt(TE, "row%d" % q)
+        sg("pb%d" % q, TE.matmul(first[q][0][:, 0:128], T.ones[0:1, :], T.rowe[0:1, c], False, True))
     wt(V, "dr")
     sg("tr", V.transpose(T.tt[:, 0:64], T.ts[:, 0:64]))
     wt(V, "i5", "tr")
     cpv("tab", T.tabr[:, :], T.tt[:, 0:64])
-    compare(T.pb1, "pb", T.oh, "ohc")
-    wt(TE, "tab", "ohc")
-    lookup("pA", T.psa, 0, T.oh, T.tabr)
-    wt(V, "pS")
-    cpv("vl0", T.l0[:, :], T.pss[:, 0:4 * M])
-    wt(V, "pA")
     for q in range(2):
-        tsc("vlf", T.lf0[:, q:48:2], T.psa[:, 24 * q:24 * q + 24], T.i24[:, q:q + 1], OP.add)
+        wt(V, "pb%d" % q)
+        tsc("oh%d" % q, T.oh[:, 128 * q:128 * q + 128], first[q][0][:, 0:128], T.kcol[:, 0:1], OP.is_equal)
+    wt(TE, "tab")
+    for q in range(2):
+        wt(TE, "oh%d" % q)
+        lookup("pA%d" % q, first[q][1], T.oh, T.tabr, q, 0)
+    wt(V, "c6")
+    for q in range(2):
+        wt(V, "pA%d" % q)
+        tsc("vlf", T.lf0[:, q:48:2], first[q][1][:, 0:24], T.i24[:, q:q + 1], OP.add)
+    wt(TE, "shx", "irp", "i6", "c4")
+    for i in range(2):
+        o = T.pss[:, 4 * HM * i:4 * HM * i + 4 * HM]
+        v = order[4 * i] % 2
+        sg("pS", TE.matmul(o, T.rp[:, 128 * v:128 * v + 128], T.shx[:, :], True, False))
+        sg("pS", TE.matmul(o, T.idb[:, :], T.cwb[:, :], False, True))
 
     H = OWN // 2
-    plan = calls(rank, T, topo)
-    relayed = routes(rank, T, topo)[1]
-    arrivals = 0
-    for src in range(NR):
-        if src != rank:
-            arrivals += sum(len(e) for call in calls(src, T, topo) for p, c, e in call if p == rank and c == core)
-            arrivals += sum(len(e) for p, e in hand_on(src, T, topo) if p == rank)
+
+    def arrivals(r, k):
+        res = 0
+        for src in range(NR):
+            if src != rank:
+                res += sum(len(e) for call in calls(src, r, k, T, topo) for p, c, e in call if p == rank and c == core)
+                res += sum(len(e) for out in hand_on(src, k, T, topo).values() for p, e in out if p == rank)
+        return res
 
     def own_chunk(r, k, win, lf):
         tag, c0 = "%d%d" % (r, k), 2 * M * k
@@ -248,19 +271,21 @@ def rank_program(g, core, T, topo):
         w, s = T["w" + tag], T["s" + tag]
         wt(V, "f" + tag)
         wt(S, "f" + tag)
-        cpv("s" + tag, s[:, 0:4 * REG], w[:, 0:OWN].indirect(T.l0[:, 0:4 * hm]))
-        cps("s" + tag, s[:, 4 * REG:8 * REG], w[:, 0:OWN].indirect(T.l0[:, 4 * hm:8 * hm]))
+        for name, a, b, c in PICKS:
+            cpv(name + tag, s[:, 16 * a:16 * b], w[:, 0:OWN].indirect(T.l0[:, a:b]))
+            cps(name + tag, s[:, 16 * b:16 * c], w[:, 0:OWN].indirect(T.l0[:, b:c]))
 
     def send(r, k):
         tag, at = "%d%d" % (r, k), OWN + REG * rank
-        wt(g, "s" + tag)
-        for call in plan:
-            tr = []
+        for call, pick in zip(calls(rank, r, k, T, topo), PICKS):
+            wt(g, pick[0] + tag)
+            tr, used = [], {}
             for p, c, e in call:
-                i = 4 * (p % 2) + p // 2
+                i = order.index(p)
                 src = T["s" + tag][:, REG * i:REG * i + REG]
-                if p in relayed:
-                    j = relayed.index(p)
+                if c != T.cores[p]:
+                    j = used.get(c, 0)
+                    used[c] = j + 1
                     tr.append(transfer(topo, c, T["rl" + tag][:, REG * j:REG * j + REG], src, T.sem["rel" + tag], e))
                 else:
                     tr.append(transfer(topo, c, T["w" + tag][:, at:at + REG], src, T.sem["arr" + tag], e))
@@ -271,127 +296,167 @@ def rank_program(g, core, T, topo):
         tag = "%d%d" % (r, k)
         w = T["w" + tag]
         for q in (V, S):
-            q.wait_ge(T.sem["arr" + tag], arrivals)
+            q.wait_ge(T.sem["arr" + tag], arrivals(r, k))
 
         def pick(j, h):
             return w[:, :].indirect(T.ln[:, 2 * M * j + M * h:2 * M * j + M * h + M])
-        halves = [(h, "ab"[h], slice(H * h, H * h + H), out[:, OWN * k + H * h:OWN * k + H * h + H]) for h in range(2)]
-        for j, s in ((0, "n"), (4, "g"), (5, "g")):
-            for h, a, c, dst in halves:
-                cps(s + a + tag, T["q%d%s" % (j, tag)][:, c], pick(j, h))
-            for h, a, c, dst in halves:
-                if j:
-                    wt(S, "g" + a + tag)
-                    if (k, j, h) == (1, 5, 0):
-                        wt(S, "vl1")
-                    if (k, j, h) == (1, 5, 1):
-                        wt(S, "aa%d0" % r)
-                    cps(("h" if j == 4 else "i") + a + tag, T[BANK[(k, j, h)]][:, 0:H], T["q%d%s" % (j, tag)][:, c])
-        for j in range(1, 6):
-            if j == 3 and middle:
-                middle()
-            for h, a, c, dst in halves:
-                wt(V, ("n" if j == 1 else "a") + a + tag)
-                if j < 4:
-                    ttn("a" + a + tag, dst, pick(j, h), T["q0" + tag][:, c] if j == 1 else dst, OP.max)
-                else:
-                    wt(V, ("h" if j == 4 else "i") + a + tag)
-                    ttn("a" + a + tag, dst, T[BANK[(k, j, h)]][:, 0:H], dst, OP.max)
 
-    wt(V, "vlf", "dx", "vl0")
-    wt(S, "vlf", "dx", "vl0")
+        def bank(i, q):
+            m = 5 * k + i
+            if m == len(BANKS) - 1:
+                wt(q, "vl1")
+            if m >= len(BANKS):
+                wt(q, "a%s%d0" % (ORDER[m - len(BANKS)][2], r))
+            return T[BANKS[m % len(BANKS)]][:, 0:H]
+
+        def part(j, h):
+            return T["q%d%s" % (j, tag)][:, H * h:H * h + H]
+
+        def dst(h):
+            return out[:, OWN * k + H * h:OWN * k + H * h + H]
+        for h in range(2):
+            cps("n" + "ab"[h] + tag, part(0, h), pick(0, h))
+        for i, (j, s, a, h) in enumerate(ORDER):
+            cps(("u" if j == 5 else "g") + s + tag, part(j, h), pick(j, h))
+            if j < 5:
+                wt(TE, "g" + s + tag)
+                b = bank(i, TE)
+                sg("h" + s + tag, TE.matmul(b, T.idf[:, :], part(j, h), True, True))
+        for i, (j, s, a, h) in enumerate(ORDER):
+            if j == 5:
+                wt(S, "u" + s + tag)
+                b = bank(i, S)
+                cps("i" + s + tag, b, part(j, h))
+        for n, (j, h) in enumerate(((1, 0), (1, 1), (2, 0), (2, 1), (3, 0))):
+            if n == 4 and middle:
+                middle()
+            a = "ab"[h]
+            wt(V, ("n" if j == 1 else "a") + a + tag)
+            ttn("a" + a + tag, dst(h), pick(j, h), part(0, h) if j == 1 else dst(h), OP.max)
+        for i in TAKE:
+            j, s, a, h = ORDER[i]
+            wt(V, "a" + a + tag, ("i" if j == 5 else "h") + s + tag)
+            ttn("a" + a + tag, dst(h), T[BANKS[(5 * k + i) % len(BANKS)]][:, 0:H], dst(h), OP.max)
+
+    wt(V, "vlf", "dx")
+    wt(S, "vlf", "dx")
     own_chunk(0, 0, T.xs, T.lf0)
+    wt(V, "pS")
+    cpv("vl0", T.l0[:, :], T.pss[:, 0:8 * HM])
+    wt(V, "vl0")
+    wt(S, "vl0")
     slots(0, 0)
-    own_chunk(0, 1, T.xs, T.lf0)
+    for k in range(1, CH):
+        own_chunk(0, k, T.xs, T.lf0)
+        slots(0, k)
+    for k in range(CH):
+        send(0, k)
+
     wt(V, "dc")
     cpv("ctb", T.tabc[:, :], T.ts[:, 64:128])
-    wt(TE, "ctb")
-    lookup("pB", T.psb, 0, T.oh, T.tabc)
+    wt(TE, "ctb", "vlf")
+    for q in range(2):
+        lookup("pB", T.psb, T.oh, T.tabc, q, 24 * q)
     wt(V, "da")
     cpv("afc", T.actf[:, :], T.acti[:, :])
     cpv("afc", T.posf[:, :], T.posi[:, :])
-    slots(0, 1)
-    send(0, 0)
-    send(0, 1)
-
+    wt(V, "dn")
+    tsc("b1", T.hi[:, :], T.nb[:, :], 3, OP.arith_shift_right)
     wt(V, "afc", "i7")
     for q in range(2):
         tsc("m1", T.mk[:, 24 * q:24 * q + 24], T.u48[:, 0:24], T.actf[:, q:q + 1], OP.is_equal)
-    wt(V, "m1", "pB")
-    ttn("m2", T.mx[:, :], T.mk[:, :], T.psb[:, 0:48], OP.mult)
-
-    def spread(mx, my, num, dg, s_in, s_num, s_dg, pb, s_pb):
-        wt(S, s_in)
-        for q in range(2):
-            c = slice(24 * q, 24 * q + 24)
-            sg(s_num, S.activation(my[:, c], mx[:, c], AF.Copy, accum_out=num[:, q:q + 1]))
-        wt(S, s_num, "i6")
-        for q in range(2):
-            sg(s_dg, S.activation(dg[:, 128 * q:128 * q + 128], T.idb[:, :], AF.Copy, scale=num[:, q:q + 1]))
-        all_rows(s_pb, pb, T.ones[:, :], dg[:, :], s_dg)
-    spread(T.mx, T.my, T.a1, T.dg2, "m2", "m3", "d2", T.pb2, "p2")
-    wt(V, "dn")
-    tsc("b1", T.hi[:, :], T.nb[:, :], 3, OP.arith_shift_right)
     tsc("b1", T.m88[:, :], T.nb[:, :], 32.0, OP.is_ge, float(REG - 8), OP.mult)
     tsc("b1", T.st0[:, :], T.nb[:, :], 32.0, OP.is_ge, -24.0, OP.mult)
-    sg("ctr", V.transpose(T.tt[:, 64:128], T.ts[:, 64:128]))
+    wt(V, "m1", "pB")
+    ttn("m2", T.mx[:, :], T.mk[:, :], T.psb[:, 0:48], OP.mult)
     wt(V, "b1")
     ttn("b2", T.hm[:, :], T.hi[:, :], T.m88[:, :], OP.mult)
     tsc("b2", T.st[:, :], T.st0[:, :], 32.0, OP.add)
-    wt(V, "ctr")
-    cpv("ctr", T.tabt[:, :], T.tt[:, 64:128])
+
+    def total(mx, num, s_in, s_num):
+        wt(V, s_in)
+        for q in range(2):
+            sg(s_num, V.tensor_reduce(num[:, q:q + 1], mx[:, 24 * q:24 * q + 24], AX.X, OP.add))
+
+    def spread(num, dg, s_num, s_dg, pb, s_pb):
+        wt(V, s_num, "i6")
+        for q in range(2):
+            tsc(s_dg, dg[:, 128 * q:128 * q + 128], T.idb[:, :], num[:, q:q + 1], OP.mult)
+        sg(s_pb, TE.matmul(pb[:, 0:256], T.ones[0:1, :], T.rcb[0:1, :], True, False))
+        wt(TE, s_dg)
+        sg(s_pb, TE.matmul(pb[:, 0:256], T.ones[:, :], dg[:, :], False, True))
+    total(T.mx, T.a1, "m2", "m3")
     wt(V, "b2")
     ttn("b6", T.base[:, :], T.hm[:, :], T.nb[:, :], OP.add)
+    sg("ctr", V.transpose(T.tt[:, 64:128], T.ts[:, 64:128]))
+    spread(T.a1, T.dg2, "m3", "d2", T.pb2, "p2")
+    wt(V, "ctr", "b6")
+    cpv("ctr", T.tabt[:, :], T.tt[:, 64:128])
+    wt(S, "zf", "ctb", "i6")
+    for t in range(2):
+        for n, (a, b, o) in ((0, (0, 16, 0)), (1, (16, 24, 0)), (1, (0, 8, 8)), (2, (8, 24, 0))):
+            z = 112 + 128 * (3 * t + n) + o
+            sg("zc", S.activation(T.zz[:, z:z + b - a], T.tabc[:, 32 * t + a:32 * t + b], AF.Copy, scale=32.0))
+    sg("idf", S.activation(T.idf[:, :], T.idb[:, :], AF.Copy))
     wt(S, "b6", "i7")
-    for n in range(6):
+    for n in range(3, 6):
+        for q in range(2):
+            j, c = 2 * n + q, 2 * M * (n - 3)
+            sg("b3", S.activation(T.lnf[:, c + q:c + 2 * M:2], T.u48[:, 0:M], AF.Identity, bias=T.base[:, j:j + 1], scale=T.st[:, j:j + 1]))
+    sg("c7", S.activation(T.r16[:, 1:2], T.r16[:, 0:1], AF.Copy, bias=16.0))
+    for q in range(2):
+        sg("c7", S.activation(T.ww[:, q:q + 1], T.w32[:, 0:1], AF.Copy, bias=1.0 - q, scale=(2.0 * q - 1.0) / 32.0))
+
+    def near_list(n):
         for q in range(2):
             j = 2 * n + q
-            sg("b3", S.activation(T.lnf[:, 2 * M * n + q:2 * M * n + 2 * M:2], T.u48[:, 0:M], AF.Identity, bias=T.base[:, j:j + 1],
-                                  scale=T.st[:, j:j + 1]))
-    compare(T.pb2, "p2", T.oh2, "o2")
+            tsc("b7", T.ln[:, 2 * M * n + q:2 * M * n + 2 * M:2], T.u48[:, 0:M], T.st[:, j:j + 1], OP.mult, T.base[:, j:j + 1], OP.add)
+    near_list(0)
+    wt(V, "p2")
+    tsc("o2", T.oh2[:, :], T.pb2[:, 0:256], T.kcol[:, 0:1], OP.is_equal)
     wt(TE, "o2", "ctr")
-    lookup("pC", T.psc, 0, T.oh2, T.tabt)
     for q in range(2):
-        tsc("c6", T.r16[:, q:q + 1], T.ri[:, 0:1], 16.0 * q, OP.add)
-        tsc("c6", T.ww[:, q:q + 1], T.wi[:, 0:1], 2.0 * q - 1.0, OP.mult, 1.0 - q, OP.add)
-    wt(V, "pC", "afc")
+        lookup("pC", T.psc, T.oh2, T.tabt, q, 24 * q)
+    near_list(1)
+    near_list(2)
+    wt(V, "pC")
     for q in range(2):
         tsc("e1", T.mk2[:, 24 * q:24 * q + 24], T.psc[:, 24 * q:24 * q + 24], T.posf[:, q:q + 1], OP.is_equal)
     wt(V, "e1")
     ttn("e2", T.mx2[:, :], T.mk2[:, :], T.u48[:, :], OP.mult)
-    spread(T.mx2, T.my2, T.k1, T.dg3, "e2", "e3", "d3", T.pb3, "p3")
-    sg("zf", V.memset(T.zz[:, :], 0.0))
-    wt(S, "zf", "ctb")
-    for t in range(2):
-        for n, (a, b, o) in ((0, (0, 16, 0)), (1, (16, 24, 0)), (1, (0, 8, 8)), (2, (8, 24, 0))):
-            z = ZW * (3 * t + n) + 112 + o
-            sg("zc", S.activation(T.zz[:, z:z + b - a], T.tabc[:, 32 * t + a:32 * t + b], AF.Copy, scale=32.0))
+    total(T.mx2, T.k1, "e2", "e3")
+    spread(T.k1, T.dg3, "e3", "d3", T.pb3, "p3")
+    for q in range(2):
+        tsc("oy", T.ohy[:, q:256:2], T.pb2[:, 128 * q:128 * q + 128], T.kcol[:, 0:1], OP.is_equal)
     wt(V, "b3")
-    cpv("b7", T.ln[:, :], T.lnf[:, :])
-    compare(T.pb3, "p3", T.oh3, "o3")
+    cpv("b7", T.ln[:, 6 * M:12 * M], T.lnf[:, :])
+    wt(V, "p3")
+    tsc("o3", T.oh3[:, :], T.pb3[:, 0:256], T.kcol[:, 0:1], OP.is_equal)
     wt(TE, "o3")
-    lookup("pD", T.psd, 0, T.oh3, T.tabc)
+    for q in range(2):
+        lookup("pD", T.psd, T.oh3, T.tabc, q, 24 * q)
 
     def next_list():
-        wt(V, "pD", "c6")
+        wt(V, "pD", "c7")
         for q in range(2):
             tsc("vl1", T.lf1[:, q:48:2], T.psd[:, 24 * q:24 * q + 24], 32.0, OP.mult, T.r16[:, q:q + 1], OP.add)
-    wt(TE, "zc", "vl0", "i7")
-    for n in range(3):
-        for q in range(2):
-            o = T.pss[:, 32 * n + 16 * q:32 * n + 16 * q + 16]
-            sg("pY", TE.matmul(o, T.ones[0:1, :], T.irow[0:1, 16 * q:16 * q + 16], True, False))
-            for gr in range(8):
-                t = gr // 4
-                z = ZW * (3 * t + n) + 112 - 16 * gr
-                c = 256 * t + 128 * q + 16 * gr
-                sg("pY", TE.matmul(o, T.zz[:, z:z + 128], T.oh2[:, c:c + 16], False, gr == 7))
+
+    def y_list(n):
+        o = T.pss[:, 32 * n:32 * n + 32]
+        sg("pY", TE.matmul(o, T.ones[0:1, :], T.irow[0:1, :], True, False))
+        for gr in range(8):
+            z = 112 + 128 * (3 * (gr // 4) + n) - 16 * gr
+            sg("pY", TE.matmul(o, T.zz[:, z:z + 128], T.ohy[:, 32 * gr:32 * gr + 32], False, gr == 7))
 
     wt(V, "b7", "vown")
     wt(S, "b7", "vown", "o3")
+    wt(TE, "idf")
     maxima_sems = [["a%s%d%d" % (h, r, k) for k in range(CH) for h in "ab"] for r in range(2)]
-    maxima(0, 0, T.n0, next_list)
-    maxima(0, 1, T.n0)
+    for k in range(CH):
+        maxima(0, k, T.n0, None if k else next_list)
+    wt(TE, "zc", "vl0", "i7", "oy")
+    for n in range(3):
+        y_list(n)
     wt(V, "vl1", *maxima_sems[0])
     wt(S, "vl1", *maxima_sems[0])
     for k in range(CH):
@@ -399,11 +464,13 @@ def rank_program(g, core, T, topo):
         slots(1, k)
     for k in range(CH):
         send(1, k)
-    wt(V, "pY", "c6")
-    cpv("vly", T.ly[:, 0:48:3], T.pss[:, 0:32:2])
-    cpv("vly", T.ly[:, 2:48:3], T.pss[:, 65:96:2])
-    tsc("y1", T.ye[:, :], T.pss[:, 32:64:2], T.ww[:, 0:1], OP.mult)
-    tsc("y1", T.yo[:, :], T.pss[:, 33:64:2], T.ww[:, 1:2], OP.mult)
+    wt(V, "pY", "c7")
+    for q in range(2):
+        tsc("y1", T.ye[:, 8 * q:8 * q + 8], T.pss[:, 32 + q:64:4], T.ww[:, 0:1], OP.mult)
+        tsc("y1", T.yo[:, 8 * q:8 * q + 8], T.pss[:, 34 + q:64:4], T.ww[:, 1:2], OP.mult)
+    for q in range(2):
+        cpv("vly", T.ly[:, 24 * q:24 * q + 24:3], T.pss[:, q:32:4])
+        cpv("vly", T.ly[:, 24 * q + 2:24 * q + 24:3], T.pss[:, 66 + q:96:4])
     wt(V, "y1")
     ttn("y3", T.yt[:, :], T.ye[:, :], T.yo[:, :], OP.add)
     wt(V, "y3")

from concourse.bass import DstId, RemoteDMATransfer
from concourse.mybir import AluOpType as OP, ActivationFunctionType as AF, AxisListType as AX

NR, M, CH = 8, 12, 2
OWN, REG = 32 * M, 8 * M
WIN = OWN + NR * REG
HM = M // 2
RK = [(r, k) for r in range(2) for k in range(CH)]
NEAR = (1,)
PICKS = (("sr", HM, 2 * HM, 3 * HM), ("s", 3 * HM, 6 * HM - 2, NR * HM))
ZT = 112 + 6 * 128
BANKS = ("pb1", "pb2", "pb3", "psa", "psb", "psc", "psd")
ORDER = ((4, "b", "b", 1), (4, "a", "a", 0), (3, "c", "b", 1), (5, "a", "a", 0), (5, "b", "b", 1))
TAKE = (0, 1, 4, 3, 2)

F32, I32, U16, B16 = "float32", "int32", "uint16", "bfloat16"


def _sb(n, t):
    return ("sbuf", [128, n], t)


SCRATCH = {
    "xs": _sb(768, F32), "n0": _sb(768, F32), "n1": _sb(768, F32), "ys": _sb(768, F32),
    "ts": _sb(128, I32), "tt": _sb(128, I32), "tabr": _sb(64, B16), "tabc": _sb(64, B16), "tabt": _sb(64, B16),
    "prow": _sb(256, I32), "rowe": _sb(256, B16), "shi": _sb(4, I32), "shf": _sb(4, F32), "shx": _sb(4 * HM, B16),
    "nb": _sb(12, I32), "acti": _sb(2, I32), "posi": _sb(2, I32), "actf": _sb(2, F32), "posf": _sb(2, F32),
    "ones": _sb(128, B16), "idb": _sb(128, B16), "idf": _sb(128, F32), "rp": _sb(256, B16),
    "pidx": _sb(2, I32), "ri": _sb(2, I32), "wi": _sb(2, I32), "i24": _sb(2, F32), "r16": _sb(2, F32), "w32": _sb(2, F32), "ww": _sb(2, F32),
    "kcol": _sb(2, F32), "rcb": _sb(256, B16), "irow": _sb(32, B16), "cwi": _sb(4 * HM, F32), "cwb": _sb(4 * HM, B16), "u48": _sb(48, F32),
    "lf0": _sb(48, U16), "lf1": _sb(48, U16), "ly": _sb(48, U16), "l0": _sb(8 * HM, U16), "ln": _sb(12 * M, U16), "lnf": _sb(6 * M, F32),
    "oh": _sb(256, B16), "oh2": _sb(256, B16), "ohy": _sb(256, B16), "oh3": _sb(256, B16), "dg2": _sb(256, B16), "dg3": _sb(256, B16),
    "zz": _sb(ZT, B16),
    "hi": _sb(12, I32), "m88": _sb(12, F32), "st0": _sb(12, F32), "st": _sb(12, F32), "hm": _sb(12, F32), "base": _sb(12, F32),
    "mk": _sb(48, F32), "mx": _sb(48, F32), "a1": _sb(2, F32),
    "mk2": _sb(48, F32), "mx2": _sb(48, F32), "k1": _sb(2, F32), "ye": _sb(16, F32), "yo": _sb(16, F32), "yt": _sb(16, F32),
}
for _n in ("pss",) + BANKS:
    SCRATCH[_n] = ("psum", [128, 512], F32)
SEMAPHORES = ["ms", "mt", "one", "zf", "vown", "i1", "i3", "i4", "i5", "i6", "i7", "irp", "c1", "c2", "c4", "c6", "c7",
              "dp", "ds", "dr", "dx", "dc", "da", "dn", "dy", "row0", "row1", "pb0", "pb1", "shc", "shx", "pS", "tr", "tab",
              "oh0", "oh1", "pA0", "pA1", "pB", "vl0", "vlf",
              "ctr", "ctb", "afc", "m1", "m2", "m3", "d2", "p2", "o2", "oy", "pC", "vly", "e1", "e2", "e3", "d3", "p3", "o3", "pD", "vl1",
              "b1", "b2", "b3", "b6", "b7", "idf", "zc", "pY", "y1", "y3", "y2a", "y2b", "lsem"]
for _r, _k in RK:
    SCRATCH["w%d%d" % (_r, _k)] = _sb(WIN, F32)
    SCRATCH["s%d%d" % (_r, _k)] = _sb(NR * REG, F32)
    SCRATCH["rl%d%d" % (_r, _k)] = _sb(2 * REG, F32)
    for _j in (0, 3, 4, 5):
        SCRATCH["q%d%d%d" % (_j, _r, _k)] = _sb(OWN, F32)
    SEMAPHORES += [_s + "%d%d" % (_r, _k) for _s in ("f", "sr", "s", "arr", "rel", "na", "nb", "aa", "ab", "ga", "gb", "gc", "ha", "hb", "hc",
                                                     "ua", "ub", "ia", "ib")]


def routes(src, k, T, topo):
    cores = T.cores
    c = cores[src]
    here = [p for p in range(NR) if p != src and topo.chip(cores[p]) == topo.chip(c)]
    away = [p for p in range(NR) if p != src and p not in here]

    def place(p):
        return sum(1 for q in range(p) if topo.chip(cores[q]) == topo.chip(cores[p]))
    same = [p for p in away if place(p) == place(src)]
    near = [p for p in same if topo.same_plane(topo.chip(c), topo.chip(cores[p]))]
    far = [p for p in same if p not in near]
    others = [h for h in topo.cores_of(c) if topo.die(h) != topo.die(c)]
    owners = [h for h in others if all(topo.may_write(h, cores[p]) for p in far)]
    plain = [h for h in others if h not in owners]
    handed = {owners[place(src)]: far}
    if k in NEAR:
        handed[plain[place(src)]] = near
    return [p for p in away if not any(p in v for v in handed.values())], handed, here


def calls(src, r, k, T, topo):
    cores = T.cores
    direct, handed, here = routes(src, k, T, topo)
    c = cores[src]
    off = topo.engines(c, cores[direct[0]])
    rest = [e for e in topo.engines(c, cores[here[0]]) if e not in off]
    first, second = [], [(p, cores[p], off[2 * i:2 * i + 2]) for i, p in enumerate(direct)]
    second += [(p, cores[p], off[2 * len(direct):] or rest) for p in here]
    for n, (h, ranks) in enumerate(handed.items()):
        use = topo.engines(c, h) if n == 0 and (r, k) == (1, 0) else rest
        m = len(use) // len(ranks)
        (second if n else first).extend((p, h, use[m * i:m * i + m]) for i, p in enumerate(ranks))
    return [first, second]


def hand_on(src, k, T, topo):
    res = {}
    for h, ranks in routes(src, k, T, topo)[1].items():
        off = topo.engines(h, T.cores[ranks[0]])
        n = len(off) // len(ranks)
        res[h] = [(p, off[n * i:n * i + n]) for i, p in enumerate(ranks)]
    return res


def transfer(topo, dst, out, src, sem, engines):
    rid, pid, _ = topo.addr(dst)
    return RemoteDMATransfer(dst_ids=[DstId(rid=rid, pnc=pid)], dma_engine_mask=sum(1 << e for e in engines), remote_sem=sem, src=src, dst=out)


def helper_program(g, core, T, topo):
    sent = 0
    for r, k in RK:
        tag = "%d%d" % (r, k)
        for src in range(NR):
            out = hand_on(src, k, T, topo).get(core)
            if not out:
                continue
            g.wait_ge(T.sem["rel" + tag], sum(len(e) for call in calls(src, r, k, T, topo) for p, c, e in call if c == core))
            at = OWN + REG * src
            g.remote_dma_fused([transfer(topo, T.cores[p], T["w" + tag][:, at:at + REG], T["rl" + tag][:, REG * i:REG * i + REG],
                                         T.sem["arr" + tag], e) for i, (p, e) in enumerate(out)], local_sem=T.sem["lsem"])
            sent += sum(len(e) for p, e in out)
    if sent:
        g.wait_ge(T.sem["lsem"], sent)


def rank_program(g, core, T, topo):
    rank = T.rank_of(core)
    if rank is None:
        helper_program(g, core, T, topo)
        return
    V, S, TE, Y = g.vector, g.scalar, g.tensor, g.sync
    cnt, seen = {}, {}

    def sg(name, inst, n=1):
        inst.then_inc(T.sem[name], n)
        cnt[name] = cnt.get(name, 0) + n

    def wt(q, *names):
        for name in names:
            q.wait_ge(T.sem[name], cnt[name])
            seen[name] = cnt[name]

    def tsc(sem, out, in0, s1, op0, s2=None, op1=None):
        if op1 is None:
            sg(sem, V.tensor_scalar(out, in0, s1, None, op0))
        else:
            sg(sem, V.tensor_scalar(out, in0, s1, s2, op0, op1))

    def ttn(sem, out, a, b, op):
        sg(sem, V.tensor_tensor(out, a, b, op))

    def cpv(sem, out, a):
        sg(sem, V.tensor_copy(out, a))

    def cps(sem, out, a):
        sg(sem, S.activation(out, a, AF.Copy))

    sg("ms", V.memset(T.ts[:, 0:64], 0))
    sg("one", V.memset(T.ones[:, :], 1.0))
    sg("mt", V.memset(T.ts[:, 64:128], 0))
    sg("dp", Y.dma_start(T.prow[0:1, 0:256], T.pose[:, :]), 16)
    sg("ds", S.dma_start(T.shi[:, :], T.shown[:, :]), 16)
    wt(Y, "ms")
    wt(S, "ms")
    for t in range(2):
        for gg in range(4):
            q = Y if gg < 2 else S
            sg("dr", q.dma_start(T.ts[32 * gg:32 * gg + 24, 32 * t:32 * t + 24], T.rel[4 * t + gg:4 * t + gg + 1, :]), 16)
    sg("dx", S.dma_start(T.xs[:, :], T.x[:, :]), 16)
    wt(Y, "mt")
    for t in range(2):
        for gg in range(4):
            sg("dc", Y.dma_start(T.ts[32 * gg:32 * gg + 24, 64 + 32 * t:64 + 32 * t + 24], T.ct[4 * t + gg:4 * t + gg + 1, :]), 16)
    sg("da", Y.dma_start(T.posi[:, :], T.pose[:, :]), 16)
    sg("da", Y.dma_start(T.acti[:, :], T.act[:, :]), 16)
    sg("dn", S.dma_start(T.nb[:, :], T.nbr[:, :]), 16)

    def iota(sem, out, pattern, cm, flag=True):
        if flag:
            sg(sem, g.iota(out, pattern, 0, cm, allow_small_or_imprecise_dtypes=True))
        else:
            sg(sem, g.iota(out, pattern, 0, cm))
    iota("i1", T.pidx[:, 0:1], [[0, 1]], 1, False)
    iota("i4", T.cwi[:, :], [[0, 4], [64, HM]], 0)
    iota("i5", T.kcol[:, 0:1], [[0, 1]], 1)
    iota("i3", T.rcb[0:1, :], [[0, 4], [32, 4], [0, 16]], 0)
    wt(g, "one")
    for v in range(2):
        sg("irp", g.affine_select(T.rp[:, 128 * v:128 * v + 128], T.ones[:, :], [[-16, 8], [0, 2], [-1, 8]], OP.is_equal, 0.0, -8 * v, 1))
    sg("i6", g.affine_select(T.idb[:, :], T.ones[:, :], [[-1, 128]], OP.is_equal, 0.0, 0, 1))
    iota("i7", T.u48[:, :], [[0, 2], [1, 24]], 0)
    iota("i7", T.irow[0:1, :], [[1, 16], [16, 2]], 0)
    for r, k in RK:
        at = OWN + REG * rank
        iota("vown", T["w%d%d" % (r, k)][:, at:at + REG], [[0, REG]], 0)

    wt(V, "i1")
    p1 = T.pidx[:, 0:1]
    tsc("c1", T.ri[:, 0:1], p1, 15, OP.bitwise_and)
    tsc("c1", T.wi[:, 0:1], p1, 3, OP.arith_shift_right, 1, OP.bitwise_and)
    sg("zf", V.memset(T.zz[:, :], 0.0))
    wt(V, "c1")
    cpv("c2", T.r16[:, 0:1], T.ri[:, 0:1])
    tsc("c2", T.w32[:, 0:1], T.wi[:, 0:1], 32.0, OP.mult)
    wt(V, "c2", "i4")
    tsc("c4", T.cwb[:, :], T.cwi[:, :], T.w32[:, 0:1], OP.add)
    wt(S, "c2")
    for q in range(2):
        sg("c6", S.activation(T.i24[:, q:q + 1], T.r16[:, 0:1], AF.Copy, bias=384.0 * q, scale=24.0))

    wt(V, "dp")
    for q in range(2):
        cpv("row%d" % q, T.rowe[0:1, 128 * q:128 * q + 128], T.prow[0:1, q:256:2])
    wt(V, "ds")
    cpv("shc", T.shf[:, :], T.shi[:, :])
    js = [rank // 2] + [p // 2 for v in routes(rank, 0, T, topo)[1].values() for p in v]
    js += [j for j in range(NR // 2) if j not in js]
    order = [2 * j + v for v in (rank % 2, 1 - rank % 2) for j in js]
    wt(S, "shc", "one")
    for i, j in enumerate(js):
        sg("shx", S.activation(T.shx[:, i * HM:i * HM + HM], T.ones[:, 0:HM], AF.Copy, scale=T.shf[:, j:j + 1]))

    def lookup(sem, ps, oh, tab, q, at):
        for t in range(2):
            sg(sem, TE.matmul(ps[64 * t:64 * t + 64, at:at + 24], oh[:, 128 * q + 64 * t:128 * q + 64 * t + 64],
                              tab[:, 32 * t:32 * t + 24], True, True))
    first = ((T.pb1, T.psa), (T.pb2, T.psc))
    wt(TE, "one", "i3")
    for q in range(2):
        c = slice(128 * q, 128 * q + 128)
        sg("pb%d" % q, TE.matmul(first[q][0][:, 0:128], T.ones[0:1, :], T.rcb[0:1, c], True, False))
    for q in range(2):
        c = slice(128 * q, 128 * q + 128)
        wt(TE, "row%d" % q)
        sg("pb%d" % q, TE.matmul(first[q][0][:, 0:128], T.ones[0:1, :], T.rowe[0:1, c], False, True))
    wt(V, "dr")
    sg("tr", V.transpose(T.tt[:, 0:64], T.ts[:, 0:64]))
    wt(V, "i5", "tr")
    cpv("tab", T.tabr[:, :], T.tt[:, 0:64])
    for q in range(2):
        wt(V, "pb%d" % q)
        tsc("oh%d" % q, T.oh[:, 128 * q:128 * q + 128], first[q][0][:, 0:128], T.kcol[:, 0:1], OP.is_equal)
    wt(TE, "tab")
    for q in range(2):
        wt(TE, "oh%d" % q)
        lookup("pA%d" % q, first[q][1], T.oh, T.tabr, q, 0)
    wt(V, "c6")
    for q in range(2):
        wt(V, "pA%d" % q)
        tsc("vlf", T.lf0[:, q:48:2], first[q][1][:, 0:24], T.i24[:, q:q + 1], OP.add)
    wt(TE, "shx", "irp", "i6", "c4")
    for i in range(2):
        o = T.pss[:, 4 * HM * i:4 * HM * i + 4 * HM]
        v = order[4 * i] % 2
        sg("pS", TE.matmul(o, T.rp[:, 128 * v:128 * v + 128], T.shx[:, :], True, False))
        sg("pS", TE.matmul(o, T.idb[:, :], T.cwb[:, :], False, True))

    H = OWN // 2

    def arrivals(r, k):
        res = 0
        for src in range(NR):
            if src != rank:
                res += sum(len(e) for call in calls(src, r, k, T, topo) for p, c, e in call if p == rank and c == core)
                res += sum(len(e) for out in hand_on(src, k, T, topo).values() for p, e in out if p == rank)
        return res

    def own_chunk(r, k, win, lf):
        tag, c0 = "%d%d" % (r, k), 2 * M * k
        w = T["w" + tag]
        cpv("f" + tag, w[:, 0:H], win[:, :].indirect(lf[:, c0:c0 + M]))
        cps("f" + tag, w[:, H:OWN], win[:, :].indirect(lf[:, c0 + M:c0 + 2 * M]))

    def slots(r, k):
        tag = "%d%d" % (r, k)
        w, s = T["w" + tag], T["s" + tag]
        wt(V, "f" + tag)
        wt(S, "f" + tag)
        for name, a, b, c in PICKS:
            cpv(name + tag, s[:, 16 * a:16 * b], w[:, 0:OWN].indirect(T.l0[:, a:b]))
            cps(name + tag, s[:, 16 * b:16 * c], w[:, 0:OWN].indirect(T.l0[:, b:c]))

    def send(r, k):
        tag, at = "%d%d" % (r, k), OWN + REG * rank
        for call, pick in zip(calls(rank, r, k, T, topo), PICKS):
            wt(g, pick[0] + tag)
            tr, used = [], {}
            for p, c, e in call:
                i = order.index(p)
                src = T["s" + tag][:, REG * i:REG * i + REG]
                if c != T.cores[p]:
                    j = used.get(c, 0)
                    used[c] = j + 1
                    tr.append(transfer(topo, c, T["rl" + tag][:, REG * j:REG * j + REG], src, T.sem["rel" + tag], e))
                else:
                    tr.append(transfer(topo, c, T["w" + tag][:, at:at + REG], src, T.sem["arr" + tag], e))
                cnt["lsem"] = cnt.get("lsem", 0) + len(e)
            g.remote_dma_fused(tr, local_sem=T.sem["lsem"])

    def maxima(r, k, out, middle=None):
        tag = "%d%d" % (r, k)
        w = T["w" + tag]
        for q in (V, S):
            q.wait_ge(T.sem["arr" + tag], arrivals(r, k))

        def pick(j, h):
            return w[:, :].indirect(T.ln[:, 2 * M * j + M * h:2 * M * j + M * h + M])

        def bank(i, q):
            m = 5 * k + i
            if m == len(BANKS) - 1:
                wt(q, "vl1")
            if m >= len(BANKS):
                wt(q, "a%s%d0" % (ORDER[m - len(BANKS)][2], r))
            return T[BANKS[m % len(BANKS)]][:, 0:H]

        def part(j, h):
            return T["q%d%s" % (j, tag)][:, H * h:H * h + H]

        def dst(h):
            return out[:, OWN * k + H * h:OWN * k + H * h + H]
        for h in range(2):
            cps("n" + "ab"[h] + tag, part(0, h), pick(0, h))
        for i, (j, s, a, h) in enumerate(ORDER):
            cps(("u" if j == 5 else "g") + s + tag, part(j, h), pick(j, h))
            if j < 5:
                wt(TE, "g" + s + tag)
                b = bank(i, TE)
                sg("h" + s + tag, TE.matmul(b, T.idf[:, :], part(j, h), True, True))
        for i, (j, s, a, h) in enumerate(ORDER):
            if j == 5:
                wt(S, "u" + s + tag)
                b = bank(i, S)
                cps("i" + s + tag, b, part(j, h))
        for n, (j, h) in enumerate(((1, 0), (1, 1), (2, 0), (2, 1), (3, 0))):
            if n == 4 and middle:
                middle()
            a = "ab"[h]
            wt(V, ("n" if j == 1 else "a") + a + tag)
            ttn("a" + a + tag, dst(h), pick(j, h), part(0, h) if j == 1 else dst(h), OP.max)
        for i in TAKE:
            j, s, a, h = ORDER[i]
            wt(V, "a" + a + tag, ("i" if j == 5 else "h") + s + tag)
            ttn("a" + a + tag, dst(h), T[BANKS[(5 * k + i) % len(BANKS)]][:, 0:H], dst(h), OP.max)

    wt(V, "vlf", "dx")
    wt(S, "vlf", "dx")
    own_chunk(0, 0, T.xs, T.lf0)
    wt(V, "pS")
    cpv("vl0", T.l0[:, :], T.pss[:, 0:8 * HM])
    wt(V, "vl0")
    wt(S, "vl0")
    slots(0, 0)
    for k in range(1, CH):
        own_chunk(0, k, T.xs, T.lf0)
        slots(0, k)
    for k in range(CH):
        send(0, k)

    wt(V, "dc")
    cpv("ctb", T.tabc[:, :], T.ts[:, 64:128])
    wt(TE, "ctb", "vlf")
    for q in range(2):
        lookup("pB", T.psb, T.oh, T.tabc, q, 24 * q)
    wt(V, "da")
    cpv("afc", T.actf[:, :], T.acti[:, :])
    cpv("afc", T.posf[:, :], T.posi[:, :])
    wt(V, "dn")
    tsc("b1", T.hi[:, :], T.nb[:, :], 3, OP.arith_shift_right)
    wt(V, "afc", "i7")
    for q in range(2):
        tsc("m1", T.mk[:, 24 * q:24 * q + 24], T.u48[:, 0:24], T.actf[:, q:q + 1], OP.is_equal)
    tsc("b1", T.m88[:, :], T.nb[:, :], 32.0, OP.is_ge, float(REG - 8), OP.mult)
    tsc("b1", T.st0[:, :], T.nb[:, :], 32.0, OP.is_ge, -24.0, OP.mult)
    wt(V, "m1", "pB")
    ttn("m2", T.mx[:, :], T.mk[:, :], T.psb[:, 0:48], OP.mult)
    wt(V, "b1")
    ttn("b2", T.hm[:, :], T.hi[:, :], T.m88[:, :], OP.mult)
    tsc("b2", T.st[:, :], T.st0[:, :], 32.0, OP.add)

    def total(mx, num, s_in, s_num):
        wt(V, s_in)
        for q in range(2):
            sg(s_num, V.tensor_reduce(num[:, q:q + 1], mx[:, 24 * q:24 * q + 24], AX.X, OP.add))

    def spread(num, dg, s_num, s_dg, pb, s_pb):
        wt(V, s_num, "i6")
        for q in range(2):
            tsc(s_dg, dg[:, 128 * q:128 * q + 128], T.idb[:, :], num[:, q:q + 1], OP.mult)
        sg(s_pb, TE.matmul(pb[:, 0:256], T.ones[0:1, :], T.rcb[0:1, :], True, False))
        wt(TE, s_dg)
        sg(s_pb, TE.matmul(pb[:, 0:256], T.ones[:, :], dg[:, :], False, True))
    total(T.mx, T.a1, "m2", "m3")
    wt(V, "b2")
    ttn("b6", T.base[:, :], T.hm[:, :], T.nb[:, :], OP.add)
    sg("ctr", V.transpose(T.tt[:, 64:128], T.ts[:, 64:128]))
    spread(T.a1, T.dg2, "m3", "d2", T.pb2, "p2")
    wt(V, "ctr", "b6")
    cpv("ctr", T.tabt[:, :], T.tt[:, 64:128])
    wt(S, "zf", "ctb", "i6")
    for t in range(2):
        for n, (a, b, o) in ((0, (0, 16, 0)), (1, (16, 24, 0)), (1, (0, 8, 8)), (2, (8, 24, 0))):
            z = 112 + 128 * (3 * t + n) + o
            sg("zc", S.activation(T.zz[:, z:z + b - a], T.tabc[:, 32 * t + a:32 * t + b], AF.Copy, scale=32.0))
    sg("idf", S.activation(T.idf[:, :], T.idb[:, :], AF.Copy))
    wt(S, "b6", "i7")
    for n in range(3, 6):
        for q in range(2):
            j, c = 2 * n + q, 2 * M * (n - 3)
            sg("b3", S.activation(T.lnf[:, c + q:c + 2 * M:2], T.u48[:, 0:M], AF.Identity, bias=T.base[:, j:j + 1], scale=T.st[:, j:j + 1]))
    sg("c7", S.activation(T.r16[:, 1:2], T.r16[:, 0:1], AF.Copy, bias=16.0))
    for q in range(2):
        sg("c7", S.activation(T.ww[:, q:q + 1], T.w32[:, 0:1], AF.Copy, bias=1.0 - q, scale=(2.0 * q - 1.0) / 32.0))

    def near_list(n):
        for q in range(2):
            j = 2 * n + q
            tsc("b7", T.ln[:, 2 * M * n + q:2 * M * n + 2 * M:2], T.u48[:, 0:M], T.st[:, j:j + 1], OP.mult, T.base[:, j:j + 1], OP.add)
    near_list(0)
    wt(V, "p2")
    tsc("o2", T.oh2[:, :], T.pb2[:, 0:256], T.kcol[:, 0:1], OP.is_equal)
    wt(TE, "o2", "ctr")
    for q in range(2):
        lookup("pC", T.psc, T.oh2, T.tabt, q, 24 * q)
    near_list(1)
    near_list(2)
    wt(V, "pC")
    for q in range(2):
        tsc("e1", T.mk2[:, 24 * q:24 * q + 24], T.psc[:, 24 * q:24 * q + 24], T.posf[:, q:q + 1], OP.is_equal)
    wt(V, "e1")
    ttn("e2", T.mx2[:, :], T.mk2[:, :], T.u48[:, :], OP.mult)
    total(T.mx2, T.k1, "e2", "e3")
    spread(T.k1, T.dg3, "e3", "d3", T.pb3, "p3")
    for q in range(2):
        tsc("oy", T.ohy[:, q:256:2], T.pb2[:, 128 * q:128 * q + 128], T.kcol[:, 0:1], OP.is_equal)
    wt(V, "b3")
    cpv("b7", T.ln[:, 6 * M:12 * M], T.lnf[:, :])
    wt(V, "p3")
    tsc("o3", T.oh3[:, :], T.pb3[:, 0:256], T.kcol[:, 0:1], OP.is_equal)
    wt(TE, "o3")
    for q in range(2):
        lookup("pD", T.psd, T.oh3, T.tabc, q, 24 * q)

    def next_list():
        wt(V, "pD", "c7")
        for q in range(2):
            tsc("vl1", T.lf1[:, q:48:2], T.psd[:, 24 * q:24 * q + 24], 32.0, OP.mult, T.r16[:, q:q + 1], OP.add)

    def y_list(n):
        o = T.pss[:, 32 * n:32 * n + 32]
        sg("pY", TE.matmul(o, T.ones[0:1, :], T.irow[0:1, :], True, False))
        for gr in range(8):
            z = 112 + 128 * (3 * (gr // 4) + n) - 16 * gr
            sg("pY", TE.matmul(o, T.zz[:, z:z + 128], T.ohy[:, 32 * gr:32 * gr + 32], False, gr == 7))

    wt(V, "b7", "vown")
    wt(S, "b7", "vown", "o3")
    wt(TE, "idf")
    maxima_sems = [["a%s%d%d" % (h, r, k) for k in range(CH) for h in "ab"] for r in range(2)]
    for k in range(CH):
        maxima(0, k, T.n0, None if k else next_list)
    wt(TE, "zc", "vl0", "i7", "oy")
    for n in range(3):
        y_list(n)
    wt(V, "vl1", *maxima_sems[0])
    wt(S, "vl1", *maxima_sems[0])
    for k in range(CH):
        own_chunk(1, k, T.n0, T.lf1)
        slots(1, k)
    for k in range(CH):
        send(1, k)
    wt(V, "pY", "c7")
    for q in range(2):
        tsc("y1", T.ye[:, 8 * q:8 * q + 8], T.pss[:, 32 + q:64:4], T.ww[:, 0:1], OP.mult)
        tsc("y1", T.yo[:, 8 * q:8 * q + 8], T.pss[:, 34 + q:64:4], T.ww[:, 1:2], OP.mult)
    for q in range(2):
        cpv("vly", T.ly[:, 24 * q:24 * q + 24:3], T.pss[:, q:32:4])
        cpv("vly", T.ly[:, 24 * q + 2:24 * q + 24:3], T.pss[:, 66 + q:96:4])
    wt(V, "y1")
    ttn("y3", T.yt[:, :], T.ye[:, :], T.yo[:, :], OP.add)
    wt(V, "y3")
    cpv("vly", T.ly[:, 1:48:3], T.yt[:, :])
    for k in range(CH):
        maxima(1, k, T.n1)

    wt(V, "vly", *maxima_sems[1])
    wt(S, "vly", *maxima_sems[1])
    cpv("y2a", T.ys[:, 0:384], T.n1[:, :].indirect(T.ly[:, 0:24]))
    cps("y2b", T.ys[:, 384:768], T.n1[:, :].indirect(T.ly[:, 24:48]))
    wt(Y, "y2a")
    sg("dy", Y.dma_start(T.y[:, 0:384], T.ys[:, 0:384]), 16)
    wt(S, "y2b")
    sg("dy", S.dma_start(T.y[:, 384:768], T.ys[:, 384:768]), 16)
    for name in cnt:
        if seen.get(name, 0) < cnt[name]:
            wt(g, name)
